import numpy as np
import ml_dtypes


def mxq(x, axis, fmt="e4m3"):
    dtype, down = {"e4m3": (ml_dtypes.float8_e4m3fn, 7), "e5m2": (ml_dtypes.float8_e5m2, 14)}[fmt]
    v = np.moveaxis(np.asarray(x, np.float32).astype(ml_dtypes.bfloat16).astype(np.float64), axis, -1)
    blocks = v.reshape(v.shape[:-1] + (-1, 32))
    amax = np.abs(blocks).max(-1, keepdims=True)
    byte = np.maximum(np.where(amax > 0, np.frexp(amax)[1] - 1 + 127, 0) - down, 1)
    scale = np.exp2(byte - 127.0)
    codes = (blocks / scale).astype(np.float32).astype(dtype).astype(np.float64)
    return np.moveaxis((codes * scale).reshape(v.shape), -1, axis)


WIDE = False


def mx_kscale(k):
    if not WIDE:
        return np.ones(k)
    levels = np.array([10, -10, 5, -5, 0])
    if k % 512:
        return np.exp2(np.random.permutation(np.resize(levels, k // 32))).repeat(32)
    a = np.empty((k // 512, 16))
    for p in range(k // 512):
        a[p, :8] = np.random.permutation(np.resize(levels, 8))
        for g in range(8):
            far = levels[np.abs(levels - a[p, g]) >= 10]
            a[p, g + 8] = far[np.random.randint(len(far))]
    return np.exp2(a.ravel()).repeat(32)


def f64(x):
    return np.asarray(x).astype(np.float64)


def striped(idx):
    return np.tile(np.asarray(idx).reshape(-1, 16).T, (8, 1)).astype(np.uint16)


def unstriped(offs):
    return offs[:16].T.reshape(-1).astype(np.int64)


E2M1 = np.array([0.0, 0.5, 1.0, 1.5, 2.0, 3.0, 4.0, 6.0, -0.0, -0.5, -1.0, -1.5, -2.0, -3.0, -4.0, -6.0])


def pack_weight(w, fmt):
    k, n = w.shape
    w = f64(np.asarray(w, np.float32).astype(ml_dtypes.bfloat16)).reshape(k // 32, 32, n)
    amax = np.abs(w).max(1)
    if fmt == "e4m3":
        byte = np.frexp(amax)[1] - 1 + 127 - 7
    else:
        mant, ex = np.frexp(amax / 6.0)
        byte = np.where(mant > 0.5, ex, ex - 1) + 127
    byte = np.clip(np.where(amax > 0, byte, 1), 1, 254)
    scaled = (w * np.exp2(127.0 - byte)[:, None, :]).reshape(k, n).astype(np.float32)
    by_word = np.ascontiguousarray(scaled.reshape(k // 512, 128, 4, n).transpose(0, 1, 3, 2))
    if fmt == "e4m3":
        words = by_word.astype(ml_dtypes.float8_e4m3fn).view(np.uint8)
    else:
        c = by_word.astype(ml_dtypes.float4_e2m1fn).view(np.uint8) & 0xF
        words = (c[..., 0::2] | (c[..., 1::2] << 4)).reshape(k // 512, 128, 2 * n)
    return np.ascontiguousarray(words), np.ascontiguousarray(byte.astype(np.uint8).reshape(k // 512, 16, n))


def unpack_weight(words, scales, fmt):
    g, _, n = scales.shape
    words = np.ascontiguousarray(words).reshape(g, 128, n, -1)
    if fmt == "e4m3":
        vals = words.view(ml_dtypes.float8_e4m3fn).astype(np.float64)
    else:
        nib = np.empty((g, 128, n, 4), np.uint8)
        nib[..., 0::2] = words & 0xF
        nib[..., 1::2] = words >> 4
        vals = E2M1[nib]
    vals = vals * np.repeat(np.exp2(scales.astype(np.float64) - 127.0), 8, axis=1)[..., None]
    return vals.transpose(0, 1, 3, 2).reshape(g * 512, n)


D, T, I, U, J, Q = 512, 2048, 512, 1024, 256, 128


def setup_inputs():
    n = np.random.standard_normal
    idx = np.random.permutation(T)[:I]
    idx2 = np.random.permutation(U)[:J]
    fd = mx_kscale(D)
    candp = pack_weight(n((D, T)) / fd[:, None], "e2m1")
    return {
        "query": (n((D, Q)) * 0.8 / np.sqrt(D) * fd[:, None]).astype(np.float32),
        "cand_words": candp[0],
        "cand_scales": candp[1],
        "other": (n((D, U)) / fd[:, None]).astype(np.float32),
        "rc": np.tile(0.3 * n(T), (128, 1)).astype(np.float32),
        "offs": striped(idx),
        "offs2": striped(idx2),
    }


def reference(query, cand_words, cand_scales, other, rc, offs, offs2):
    idx = unstriped(offs)
    idx2 = unstriped(offs2)
    candu = unpack_weight(cand_words, cand_scales, "e2m1")
    queryq = mxq(f64(query), 0, "e4m3")
    candidxg = candu[:, idx]
    a = queryq.T @ candidxg
    otherq = mxq(f64(other), 0, "e4m3")
    b = queryq.T @ otherq
    m = np.mean(b[:, idx2], axis=1, keepdims=True)
    y = 2.0 * a - m - f64(rc)[:1][:, idx]
    return y

@@ -1,0 +1,171 @@
+from contextlib import ExitStack
+
+import concourse.mybir as mybir
+from concourse.masks import make_identity
+
+D, T, I, U, J, Q = 512, 2048, 512, 1024, 256, 128
+FLOPS = 2 * D * Q * (I + U)
+BYTES = 4 * D * Q + 2 * 128 * T + 16 * T + 4 * D * U + 4 * T + 2 * 128 * (I + J) // 16 + 4 * Q * I
+
+F32 = mybir.dt.float32
+BF16 = mybir.dt.bfloat16
+I32 = mybir.dt.int32
+U32 = mybir.dt.uint32
+U16 = mybir.dt.uint16
+U8 = mybir.dt.uint8
+FP8X4 = mybir.dt.float8_e4m3fn_x4
+FP4X4 = mybir.dt.float4_e2m1fn_x4
+ALU = mybir.AluOpType
+
+P = 128
+PACK = 4
+BANK = 512
+CHUNKS = [(256, 256), (256, 256), (256, 128), (128, 128), (128, 0)]
+
+
+def tile_attend_localscaling_kernel(tc, query, cand_words, cand_scales, other, rc, offs, offs2, out):
+    nc = tc.nc
+    with ExitStack() as ctx:
+        sb = ctx.enter_context(tc.tile_pool(name="sb", bufs=1))
+        ps = ctx.enter_context(tc.psum_pool(name="ps", bufs=1))
+
+        def interleave(engine_copy, grouped, raw, lo, hi):
+            engine_copy(
+                grouped[:, lo:hi, :].rearrange("p (c i) t -> p c t i", i=4),
+                raw[:, :, lo:hi].rearrange("p t (c i) -> p c t i", i=4),
+            )
+
+        starts = [sum(w for w, s in CHUNKS[:n]) for n in range(len(CHUNKS))]
+        offs_sb = sb.tile([P, I // 16], U16, name="offs_sb")
+        offs2_sb = sb.tile([P, J // 16], U16, name="offs2_sb")
+        q_raw = sb.tile([P, PACK, Q], F32, name="q_raw")
+        words = sb.tile([P, T], U16, name="words")
+        scales = sb.tile([P, T], U8, name="scales")
+        rc_sb = sb.tile([P, T], F32, name="rc_sb")
+        o_raw = [sb.tile([P, PACK, w], F32, name="o_raw%d" % n) for n, (w, s) in enumerate(CHUNKS)]
+
+        def load_other(n):
+            w = CHUNKS[n][0]
+            nc.sync.dma_start(o_raw[n][:], other[:, starts[n] : starts[n] + w].rearrange("(p t) u -> p t u", t=PACK))
+
+        nc.vector.memset(scales[:].bitcast(I32), 0)
+        nc.vector.memset(rc_sb[:], 0.0)
+        nc.sync.dma_start(offs_sb[:], offs)
+        nc.sync.dma_start(q_raw[:], query.rearrange("(p t) q -> p t q", t=PACK))
+        load_other(0)
+        nc.sync.dma_start(words[:].bitcast(I32), cand_words[0].bitcast(I32))
+        for quad in range(4):
+            nc.scalar.dma_start(scales[32 * quad : 32 * quad + 4, :].bitcast(I32), cand_scales[0, 4 * quad : 4 * quad + 4, :].bitcast(I32))
+        nc.scalar.dma_start(rc_sb[0:1, :], rc[0:1, :])
+        for n in range(1, len(CHUNKS)):
+            load_other(n)
+        nc.sync.dma_start(offs2_sb[:], offs2)
+        ident = sb.tile([P, P], F32, name="ident")
+        make_identity(nc, ident[:])
+
+        q_grp = sb.tile([P, Q, PACK], BF16, name="q_grp", align_bytes=64)
+        q_codes = sb.tile([P, Q], U32, name="q_codes", align_bytes=64)
+        q_scales = sb.tile([P, Q], U8, name="q_scales", align_bytes=64)
+        g_words = sb.tile([P, I], U16, name="g_words", align_bytes=64)
+        g_scales = sb.tile([P, I], U8, name="g_scales", align_bytes=64)
+        g_rc = sb.tile([P, I], F32, name="g_rc")
+        rc_cols = sb.tile([P, I // P], F32, name="rc_cols")
+        rc_all = sb.tile([P, I], F32, name="rc_all")
+        b_sb = sb.tile([P, U], F32, name="b_sb")
+        z = sb.tile([P, I], F32, name="z")
+        g_b = sb.tile([P, J], F32, name="g_b")
+        m = sb.tile([P, 1], F32, name="m")
+        res = sb.tile([P, I], F32, name="res")
+        o_grp = [sb.tile([P, w, PACK], BF16, name="o_grp%d" % n, align_bytes=64) for n, (w, s) in enumerate(CHUNKS)]
+        o_codes = [sb.tile([P, w], U32, name="o_codes%d" % n, align_bytes=64) for n, (w, s) in enumerate(CHUNKS)]
+        o_scales = [sb.tile([P, w], U8, name="o_scales%d" % n, align_bytes=64) for n, (w, s) in enumerate(CHUNKS)]
+        b_ps = [ps.tile([P, BANK], F32, name="b_ps%d" % n) for n in range(len(CHUNKS))]
+        a_ps = ps.tile([P, BANK], F32, name="a_ps")
+        col_ps = ps.tile([P, I // P, P], F32, name="col_ps")
+        row_ps = ps.tile([P, I // P, P], F32, name="row_ps")
+
+        def cast_s(n):
+            w, s = CHUNKS[n]
+            if s > 0:
+                interleave(nc.scalar.copy, o_grp[n], o_raw[n], 0, s)
+
+        def cast_v(n):
+            w, s = CHUNKS[n]
+            if s < w:
+                interleave(nc.vector.tensor_copy, o_grp[n], o_raw[n], s, w)
+
+        def quant(n):
+            nc.vector.quantize_mx(o_codes[n][:].bitcast(FP8X4), o_scales[n][:], o_grp[n][:].rearrange("p u t -> p (u t)"))
+
+        def score(n):
+            w = CHUNKS[n][0]
+            nc.tensor.matmul_mx(b_ps[n][:, :w], lhsT=q_codes[:].bitcast(FP8X4), lhsT_scale=q_scales[:],
+                                rhs=o_codes[n][:].bitcast(FP8X4), rhs_scale=o_scales[n][:], start=True, stop=True)
+
+        def evict(n):
+            w = CHUNKS[n][0]
+            nc.scalar.copy(b_sb[:, starts[n] : starts[n] + w], b_ps[n][:, :w])
+
+        def quant_q():
+            nc.vector.quantize_mx(q_codes[:].bitcast(FP8X4), q_scales[:], q_grp[:].rearrange("p u t -> p (u t)"))
+
+        def gather_scales():
+            nc.vector.tensor_copy(g_scales[:], scales[:].indirect(offs_sb[:]))
+
+        def gather_words():
+            nc.vector.tensor_copy(g_words[:], words[:].indirect(offs_sb[:]))
+
+        def gather_rc():
+            nc.vector.tensor_copy(g_rc[:], rc_sb[:].indirect(offs_sb[:]))
+
+        def rc_turn():
+            for c in range(I // P):
+                nc.tensor.transpose(col_ps[:, c, :], g_rc[:, c * P : (c + 1) * P], ident[:])
+            nc.scalar.copy(rc_cols[:], col_ps[:, :, 0])
+
+        def rc_spread():
+            for c in range(I // P):
+                nc.tensor.transpose(row_ps[:, c, :], rc_cols[:, c : c + 1].to_broadcast([P, P]), ident[:])
+            nc.scalar.copy(rc_all[:], row_ps[:].rearrange("p c i -> p (c i)"))
+
+        def score_a():
+            nc.tensor.matmul_mx(a_ps[:], lhsT=q_codes[:].bitcast(FP8X4), lhsT_scale=q_scales[:],
+                                rhs=g_words[:].bitcast(FP4X4), rhs_scale=g_scales[:], start=True, stop=True)
+
+        def make_z():
+            nc.vector.scalar_tensor_tensor(z[:], a_ps[:], 2.0, rc_all[:], ALU.mult, ALU.subtract)
+
+        interleave(nc.scalar.copy, q_grp, q_raw, 0, Q)
+        cast_s(0)
+        gather_scales()
+        gather_rc()
+        quant_q()
+        quant(0)
+        score(0)
+        rc_turn()
+        gather_words()
+        rc_spread()
+        evict(0)
+        cast_s(1)
+        score_a()
+        quant(1)
+        score(1)
+        cast_s(2)
+        cast_v(2)
+        evict(1)
+        quant(2)
+        score(2)
+        cast_s(3)
+        quant(3)
+        score(3)
+        cast_v(4)
+        evict(2)
+        quant(4)
+        score(4)
+        evict(3)
+        evict(4)
+        make_z()
+        nc.vector.tensor_copy(g_b[:], b_sb[:].indirect(offs2_sb[:]))
+        nc.vector.tensor_scalar(g_b[:], g_b[:], 1.0 / J, None, ALU.mult, ALU.add, accum_out=m[:])
+        nc.vector.tensor_scalar(res[:], z[:], m[:], None, ALU.subtract)
+        nc.sync.dma_start(out, res[:])

@@ -1,7 +1,6 @@
 from contextlib import ExitStack
 
 import concourse.mybir as mybir
-from concourse.masks import make_identity
 
 D, T, I, U, J, Q = 512, 2048, 512, 1024, 256, 128
 FLOPS = 2 * D * Q * (I + U)
@@ -16,11 +15,20 @@ U8 = mybir.dt.uint8
 FP8X4 = mybir.dt.float8_e4m3fn_x4
 FP4X4 = mybir.dt.float4_e2m1fn_x4
 ALU = mybir.AluOpType
+ACT = mybir.ActivationFunctionType
 
 P = 128
 PACK = 4
+RUN = 4
 BANK = 512
-CHUNKS = [(256, 256), (256, 256), (256, 128), (128, 128), (128, 0)]
+ALIGN = 64
+SLOT_TILES = I // P
+HALF = I // 2
+
+CHUNKS = [(256, 128), (384, 256), (0, 256), (640, 256), (896, 128)]
+BANKS = [(0, 384), (384, 896), (896, 1024)]
+BANK_OF = [0, 1, 0, 1, 2]
+EARLY = 2
 
 
 def tile_attend_localscaling_kernel(tc, query, cand_words, cand_scales, other, rc, offs, offs2, out):
@@ -29,143 +37,152 @@ def tile_attend_localscaling_kernel(tc, query, cand_words, cand_scales, other, r
         sb = ctx.enter_context(tc.tile_pool(name="sb", bufs=1))
         ps = ctx.enter_context(tc.psum_pool(name="ps", bufs=1))
 
-        def interleave(engine_copy, grouped, raw, lo, hi):
-            engine_copy(
-                grouped[:, lo:hi, :].rearrange("p (c i) t -> p c t i", i=4),
-                raw[:, :, lo:hi].rearrange("p t (c i) -> p c t i", i=4),
+        def by_word(rows):
+            return rows.rearrange("(p t) c -> p t c", t=PACK)
+
+        def interleave(copy, grouped, raw):
+            copy(
+                grouped[:].rearrange("p (c i) t -> p c t i", i=RUN),
+                raw.rearrange("p t (c i) -> p c t i", i=RUN),
             )
 
-        starts = [sum(w for w, s in CHUNKS[:n]) for n in range(len(CHUNKS))]
+        def quantise(codes, code_scales, grouped):
+            nc.vector.quantize_mx(codes[:].bitcast(FP8X4), code_scales[:], grouped[:].rearrange("p c t -> p (c t)"))
+
         offs_sb = sb.tile([P, I // 16], U16, name="offs_sb")
         offs2_sb = sb.tile([P, J // 16], U16, name="offs2_sb")
         q_raw = sb.tile([P, PACK, Q], F32, name="q_raw")
-        words = sb.tile([P, T], U16, name="words")
-        scales = sb.tile([P, T], U8, name="scales")
-        rc_sb = sb.tile([P, T], F32, name="rc_sb")
-        o_raw = [sb.tile([P, PACK, w], F32, name="o_raw%d" % n) for n, (w, s) in enumerate(CHUNKS)]
+        scales = sb.tile([P, T], U8, name="scales", align_bytes=ALIGN)
+        rc_sb = sb.tile([P, T], F32, name="rc_sb", align_bytes=ALIGN)
 
-        def load_other(n):
-            w = CHUNKS[n][0]
-            nc.sync.dma_start(o_raw[n][:], other[:, starts[n] : starts[n] + w].rearrange("(p t) u -> p t u", t=PACK))
+        nc.gpsimd.memset(scales[:].bitcast(I32), 0)
+        nc.vector.memset(rc_sb[:].bitcast(I32), 0)
 
-        nc.vector.memset(scales[:].bitcast(I32), 0)
-        nc.vector.memset(rc_sb[:], 0.0)
-        nc.sync.dma_start(offs_sb[:], offs)
-        nc.sync.dma_start(q_raw[:], query.rearrange("(p t) q -> p t q", t=PACK))
-        load_other(0)
-        nc.sync.dma_start(words[:].bitcast(I32), cand_words[0].bitcast(I32))
-        for quad in range(4):
-            nc.scalar.dma_start(scales[32 * quad : 32 * quad + 4, :].bitcast(I32), cand_scales[0, 4 * quad : 4 * quad + 4, :].bitcast(I32))
-        nc.scalar.dma_start(rc_sb[0:1, :], rc[0:1, :])
-        for n in range(1, len(CHUNKS)):
-            load_other(n)
-        nc.sync.dma_start(offs2_sb[:], offs2)
         ident = sb.tile([P, P], F32, name="ident")
-        make_identity(nc, ident[:])
+        for h, tag in enumerate(("late_other", "late_words")):
+            zeros = sb.tile([P, P // 2], F32, name="zeros%d" % h, tag=tag)
+            nc.vector.memset(zeros[:], 0.0)
+            nc.gpsimd.affine_select(
+                out=ident[:, h * P // 2 : (h + 1) * P // 2],
+                in_=zeros[:],
+                compare_op=ALU.not_equal,
+                fill=1.0,
+                base=-h * P // 2,
+                pattern=[[-1, P // 2]],
+                channel_multiplier=1,
+            )
 
-        q_grp = sb.tile([P, Q, PACK], BF16, name="q_grp", align_bytes=64)
-        q_codes = sb.tile([P, Q], U32, name="q_codes", align_bytes=64)
-        q_scales = sb.tile([P, Q], U8, name="q_scales", align_bytes=64)
-        g_words = sb.tile([P, I], U16, name="g_words", align_bytes=64)
-        g_scales = sb.tile([P, I], U8, name="g_scales", align_bytes=64)
-        g_rc = sb.tile([P, I], F32, name="g_rc")
-        rc_cols = sb.tile([P, I // P], F32, name="rc_cols")
-        rc_all = sb.tile([P, I], F32, name="rc_all")
-        b_sb = sb.tile([P, U], F32, name="b_sb")
-        z = sb.tile([P, I], F32, name="z")
-        g_b = sb.tile([P, J], F32, name="g_b")
-        m = sb.tile([P, 1], F32, name="m")
-        res = sb.tile([P, I], F32, name="res")
-        o_grp = [sb.tile([P, w, PACK], BF16, name="o_grp%d" % n, align_bytes=64) for n, (w, s) in enumerate(CHUNKS)]
-        o_codes = [sb.tile([P, w], U32, name="o_codes%d" % n, align_bytes=64) for n, (w, s) in enumerate(CHUNKS)]
-        o_scales = [sb.tile([P, w], U8, name="o_scales%d" % n, align_bytes=64) for n, (w, s) in enumerate(CHUNKS)]
-        b_ps = [ps.tile([P, BANK], F32, name="b_ps%d" % n) for n in range(len(CHUNKS))]
-        a_ps = ps.tile([P, BANK], F32, name="a_ps")
-        col_ps = ps.tile([P, I // P, P], F32, name="col_ps")
-        row_ps = ps.tile([P, I // P, P], F32, name="row_ps")
+        early_lo = CHUNKS[0][0]
+        early_width = sum(width for lo, width in CHUNKS[:EARLY])
+        early_raw = sb.tile([P, PACK, early_width], F32, name="early_raw")
+        nc.sync.dma_start(offs_sb[:], offs)
+        for quadrant in range(4):
+            nc.sync.dma_start(
+                scales[32 * quadrant : 32 * quadrant + 4, :].bitcast(I32),
+                cand_scales[0, 4 * quadrant : 4 * quadrant + 4, :].bitcast(I32),
+            )
+        nc.sync.dma_start(q_raw[:], by_word(query))
+        nc.sync.dma_start(early_raw[:], by_word(other[:, early_lo : early_lo + early_width]))
+        nc.sync.dma_start(offs2_sb[:], offs2)
+        nc.sync.dma_start(rc_sb[0:1, :], rc[0:1, :])
 
-        def cast_s(n):
-            w, s = CHUNKS[n]
-            if s > 0:
-                interleave(nc.scalar.copy, o_grp[n], o_raw[n], 0, s)
+        o_raw = [early_raw[:, :, lo - early_lo : lo - early_lo + width] for lo, width in CHUNKS[:EARLY]]
+        late_raw = sb.tile([P, PACK * (U - early_width)], F32, name="late_raw", tag="late_other")
+        at = 0
+        for lo, width in CHUNKS[EARLY:]:
+            o_raw.append(late_raw[:, at : at + PACK * width].rearrange("p (t c) -> p t c", t=PACK))
+            nc.sync.dma_start(o_raw[-1], by_word(other[:, lo : lo + width]))
+            at = at + PACK * width
+        words = sb.tile([P, T], U16, name="words", tag="late_words")
+        nc.sync.dma_start(words[:].bitcast(I32), cand_words[0].bitcast(I32))
 
-        def cast_v(n):
-            w, s = CHUNKS[n]
-            if s < w:
-                interleave(nc.vector.tensor_copy, o_grp[n], o_raw[n], s, w)
+        q_grouped = sb.tile([P, Q, PACK], BF16, name="q_grouped", align_bytes=ALIGN)
+        q_codes = sb.tile([P, Q], U32, name="q_codes", align_bytes=ALIGN)
+        q_scales = sb.tile([P, Q], U8, name="q_scales", align_bytes=ALIGN)
+        o_codes = [sb.tile([P, w], U32, name="o_codes%d" % n, align_bytes=ALIGN) for n, (lo, w) in enumerate(CHUNKS)]
+        o_scales = [sb.tile([P, w], U8, name="o_scales%d" % n, align_bytes=ALIGN) for n, (lo, w) in enumerate(CHUNKS)]
+        b_ps = [ps.tile([P, BANK], F32, name="b_ps%d" % k) for k in range(len(BANKS))]
+        a_ps = ps.tile([P, I], F32, name="a_ps")
+        rc_turned_ps = ps.tile([P, SLOT_TILES, P], F32, name="rc_turned_ps")
+        rc_rows_ps = ps.tile([P, I], F32, name="rc_rows_ps")
+        o_grouped = {}
 
-        def quant(n):
-            nc.vector.quantize_mx(o_codes[n][:].bitcast(FP8X4), o_scales[n][:], o_grp[n][:].rearrange("p u t -> p (u t)"))
+        def cast(n, copy, tag):
+            o_grouped[n] = sb.tile([P, CHUNKS[n][1], PACK], BF16, name="o_grouped%d" % n, tag=tag, align_bytes=ALIGN)
+            interleave(copy, o_grouped[n], o_raw[n])
 
-        def score(n):
-            w = CHUNKS[n][0]
-            nc.tensor.matmul_mx(b_ps[n][:, :w], lhsT=q_codes[:].bitcast(FP8X4), lhsT_scale=q_scales[:],
-                                rhs=o_codes[n][:].bitcast(FP8X4), rhs_scale=o_scales[n][:], start=True, stop=True)
+        def score_chunk(n):
+            lo, width = CHUNKS[n]
+            in_bank = lo - BANKS[BANK_OF[n]][0]
+            quantise(o_codes[n], o_scales[n], o_grouped[n])
+            nc.tensor.matmul_mx(
+                b_ps[BANK_OF[n]][:, in_bank : in_bank + width],
+                lhsT=q_codes[:].bitcast(FP8X4),
+                lhsT_scale=q_scales[:],
+                rhs=o_codes[n][:].bitcast(FP8X4),
+                rhs_scale=o_scales[n][:],
+                start=True,
+                stop=True,
+            )
 
-        def evict(n):
-            w = CHUNKS[n][0]
-            nc.scalar.copy(b_sb[:, starts[n] : starts[n] + w], b_ps[n][:, :w])
+        def empty_bank(k):
+            lo, hi = BANKS[k]
+            nc.scalar.copy(b_sb[:, lo:hi], b_ps[k][:, : hi - lo])
 
-        def quant_q():
-            nc.vector.quantize_mx(q_codes[:].bitcast(FP8X4), q_scales[:], q_grp[:].rearrange("p u t -> p (u t)"))
+        listed_scales = sb.tile([P, I], U8, name="listed_scales", align_bytes=ALIGN)
+        nc.vector.tensor_copy(listed_scales[:], scales[:].indirect(offs_sb[:]))
+        interleave(nc.vector.tensor_copy, q_grouped, q_raw[:])
+        cast(1, nc.scalar.copy, "grouped1")
+        quantise(q_codes, q_scales, q_grouped)
 
-        def gather_scales():
-            nc.vector.tensor_copy(g_scales[:], scales[:].indirect(offs_sb[:]))
+        listed_rc = sb.tile([P, I], F32, name="listed_rc", tag="scales", align_bytes=ALIGN)
+        nc.vector.tensor_copy(listed_rc[:], rc_sb[:].indirect(offs_sb[:]))
+        for c in range(SLOT_TILES):
+            nc.tensor.transpose(rc_turned_ps[:, c, :], listed_rc[:, c * P : (c + 1) * P], ident[:])
 
-        def gather_words():
-            nc.vector.tensor_copy(g_words[:], words[:].indirect(offs_sb[:]))
+        cast(0, nc.vector.tensor_copy, "rc_sb")
+        score_chunk(0)
+        score_chunk(1)
+        cast(2, nc.scalar.copy, "grouped2")
+        cast(3, nc.scalar.copy, "grouped3")
+        score_chunk(2)
+        cast(4, nc.vector.tensor_copy, "grouped2")
+        b_sb = sb.tile([P, U], F32, name="b_sb", tag="late_other")
+        empty_bank(0)
+        score_chunk(3)
+        score_chunk(4)
+        empty_bank(1)
+        empty_bank(2)
 
-        def gather_rc():
-            nc.vector.tensor_copy(g_rc[:], rc_sb[:].indirect(offs_sb[:]))
+        rc_repeated = sb.tile([P, SLOT_TILES, P], F32, name="rc_repeated", tag="grouped3", align_bytes=ALIGN)
+        nc.scalar.copy(rc_repeated[:], rc_turned_ps[:, :, 0:1].to_broadcast([P, SLOT_TILES, P]))
+        for c in range(SLOT_TILES):
+            nc.tensor.transpose(rc_rows_ps[:, c * P : (c + 1) * P], rc_repeated[:, c, :], ident[:])
 
-        def rc_turn():
-            for c in range(I // P):
-                nc.tensor.transpose(col_ps[:, c, :], g_rc[:, c * P : (c + 1) * P], ident[:])
-            nc.scalar.copy(rc_cols[:], col_ps[:, :, 0])
+        listed_words = sb.tile([P, I], U16, name="listed_words", tag="grouped2", align_bytes=ALIGN)
+        nc.vector.tensor_copy(listed_words[:], words[:].indirect(offs_sb[:]))
+        nc.tensor.matmul_mx(
+            a_ps[:],
+            lhsT=q_codes[:].bitcast(FP8X4),
+            lhsT_scale=q_scales[:],
+            rhs=listed_words[:].bitcast(FP4X4),
+            rhs_scale=listed_scales[:],
+            start=True,
+            stop=True,
+        )
+        halves = [slice(h * HALF, (h + 1) * HALF) for h in range(2)]
+        twice_a = [sb.tile([P, HALF], F32, name="twice_a%d" % h) for h in range(2)]
+        for h in range(2):
+            nc.scalar.activation(twice_a[h][:], a_ps[:, halves[h]], ACT.Copy, scale=2.0)
 
-        def rc_spread():
-            for c in range(I // P):
-                nc.tensor.transpose(row_ps[:, c, :], rc_cols[:, c : c + 1].to_broadcast([P, P]), ident[:])
-            nc.scalar.copy(rc_all[:], row_ps[:].rearrange("p c i -> p (c i)"))
+        listed_b = sb.tile([P, J], F32, name="listed_b")
+        neg_mean = sb.tile([P, 1], F32, name="neg_mean")
+        nc.vector.tensor_copy(listed_b[:], b_sb[:].indirect(offs2_sb[:]))
+        nc.vector.tensor_scalar(listed_b[:], listed_b[:], -1.0 / J, None, ALU.mult, ALU.add, accum_out=neg_mean[:])
 
-        def score_a():
-            nc.tensor.matmul_mx(a_ps[:], lhsT=q_codes[:].bitcast(FP8X4), lhsT_scale=q_scales[:],
-                                rhs=g_words[:].bitcast(FP4X4), rhs_scale=g_scales[:], start=True, stop=True)
-
-        def make_z():
-            nc.vector.scalar_tensor_tensor(z[:], a_ps[:], 2.0, rc_all[:], ALU.mult, ALU.subtract)
-
-        interleave(nc.scalar.copy, q_grp, q_raw, 0, Q)
-        cast_s(0)
-        gather_scales()
-        gather_rc()
-        quant_q()
-        quant(0)
-        score(0)
-        rc_turn()
-        gather_words()
-        rc_spread()
-        evict(0)
-        cast_s(1)
-        score_a()
-        quant(1)
-        score(1)
-        cast_s(2)
-        cast_v(2)
-        evict(1)
-        quant(2)
-        score(2)
-        cast_s(3)
-        quant(3)
-        score(3)
-        cast_v(4)
-        evict(2)
-        quant(4)
-        score(4)
-        evict(3)
-        evict(4)
-        make_z()
-        nc.vector.tensor_copy(g_b[:], b_sb[:].indirect(offs2_sb[:]))
-        nc.vector.tensor_scalar(g_b[:], g_b[:], 1.0 / J, None, ALU.mult, ALU.add, accum_out=m[:])
-        nc.vector.tensor_scalar(res[:], z[:], m[:], None, ALU.subtract)
-        nc.sync.dma_start(out, res[:])
+        for h in range(2):
+            result = sb.tile([P, HALF], F32, name="result%d" % h)
+            nc.vector.scalar_tensor_tensor(
+                result[:], twice_a[h][:], neg_mean[:], rc_rows_ps[:, halves[h]], ALU.add, ALU.subtract
+            )
+            nc.sync.dma_start(out[:, halves[h]], result[:])

@@ -1,6 +1,7 @@
 from contextlib import ExitStack
 
 import concourse.mybir as mybir
+from concourse.masks import make_identity
 
 D, T, I, U, J, Q = 512, 2048, 512, 1024, 256, 128
 FLOPS = 2 * D * Q * (I + U)
@@ -25,10 +26,13 @@ ALIGN = 64
 SLOT_TILES = I // P
 HALF = I // 2
 
-CHUNKS = [(256, 128), (384, 256), (0, 256), (640, 256), (896, 128)]
-BANKS = [(0, 384), (384, 896), (896, 1024)]
-BANK_OF = [0, 1, 0, 1, 2]
-EARLY = 2
+LOADS = [(0, 256), (256, 384), (640, 256), (896, 128)]
+CHUNKS = [(0, 0, 256, 0), (1, 256, 256, 256), (1, 512, 128, 0), (2, 640, 256, 128), (3, 896, 128, 128)]
+BANKS = [(0, 256), (256, 640), (640, 896), (896, 1024)]
+BANK_OF = [0, 1, 1, 2, 3]
+RC_ROW = P - 1
+BLOCKS = D // 32
+SCALE_ROW = 48
 
 
 def tile_attend_localscaling_kernel(tc, query, cand_words, cand_scales, other, rc, offs, offs2, out):
@@ -42,7 +46,7 @@ def tile_attend_localscaling_kernel(tc, query, cand_words, cand_scales, other, r
 
         def interleave(copy, grouped, raw):
             copy(
-                grouped[:].rearrange("p (c i) t -> p c t i", i=RUN),
+                grouped.rearrange("p (c i) t -> p c t i", i=RUN),
                 raw.rearrange("p t (c i) -> p c t i", i=RUN),
             )
 
@@ -55,64 +59,47 @@ def tile_attend_localscaling_kernel(tc, query, cand_words, cand_scales, other, r
         scales = sb.tile([P, T], U8, name="scales", align_bytes=ALIGN)
         rc_sb = sb.tile([P, T], F32, name="rc_sb", align_bytes=ALIGN)
 
-        nc.gpsimd.memset(scales[:].bitcast(I32), 0)
-        nc.vector.memset(rc_sb[:].bitcast(I32), 0)
-
+        nc.vector.memset(rc_sb[0:RC_ROW, :].bitcast(I32), 0)
+        nc.gpsimd.memset(scales[0:SCALE_ROW, :].bitcast(I32), 0)
+        nc.gpsimd.memset(scales[SCALE_ROW + BLOCKS : P, :].bitcast(I32), 0)
         ident = sb.tile([P, P], F32, name="ident")
-        for h, tag in enumerate(("late_other", "late_words")):
-            zeros = sb.tile([P, P // 2], F32, name="zeros%d" % h, tag=tag)
-            nc.vector.memset(zeros[:], 0.0)
-            nc.gpsimd.affine_select(
-                out=ident[:, h * P // 2 : (h + 1) * P // 2],
-                in_=zeros[:],
-                compare_op=ALU.not_equal,
-                fill=1.0,
-                base=-h * P // 2,
-                pattern=[[-1, P // 2]],
-                channel_multiplier=1,
-            )
+        make_identity(nc, ident[:])
+        listed_scales = sb.tile([P, I], U8, name="listed_scales", align_bytes=ALIGN)
+        nc.gpsimd.memset(listed_scales[:].bitcast(I32), 0)
 
-        early_lo = CHUNKS[0][0]
-        early_width = sum(width for lo, width in CHUNKS[:EARLY])
-        early_raw = sb.tile([P, PACK, early_width], F32, name="early_raw")
         nc.sync.dma_start(offs_sb[:], offs)
-        for quadrant in range(4):
-            nc.sync.dma_start(
-                scales[32 * quadrant : 32 * quadrant + 4, :].bitcast(I32),
-                cand_scales[0, 4 * quadrant : 4 * quadrant + 4, :].bitcast(I32),
-            )
+        nc.sync.dma_start(rc_sb[RC_ROW:P, :], rc[0:1, :])
+        nc.sync.dma_start(scales[SCALE_ROW : SCALE_ROW + BLOCKS, :].bitcast(I32), cand_scales[0].bitcast(I32))
         nc.sync.dma_start(q_raw[:], by_word(query))
-        nc.sync.dma_start(early_raw[:], by_word(other[:, early_lo : early_lo + early_width]))
         nc.sync.dma_start(offs2_sb[:], offs2)
-        nc.sync.dma_start(rc_sb[0:1, :], rc[0:1, :])
-
-        o_raw = [early_raw[:, :, lo - early_lo : lo - early_lo + width] for lo, width in CHUNKS[:EARLY]]
-        late_raw = sb.tile([P, PACK * (U - early_width)], F32, name="late_raw", tag="late_other")
-        at = 0
-        for lo, width in CHUNKS[EARLY:]:
-            o_raw.append(late_raw[:, at : at + PACK * width].rearrange("p (t c) -> p t c", t=PACK))
-            nc.sync.dma_start(o_raw[-1], by_word(other[:, lo : lo + width]))
-            at = at + PACK * width
-        words = sb.tile([P, T], U16, name="words", tag="late_words")
+        o_raw = []
+        for n, (lo, width) in enumerate(LOADS):
+            o_raw.append(sb.tile([P, PACK, width], F32, name="o_raw%d" % n))
+            nc.sync.dma_start(o_raw[-1][:], by_word(other[:, lo : lo + width]))
+        words = sb.tile([P, T], U16, name="words")
         nc.sync.dma_start(words[:].bitcast(I32), cand_words[0].bitcast(I32))
 
         q_grouped = sb.tile([P, Q, PACK], BF16, name="q_grouped", align_bytes=ALIGN)
         q_codes = sb.tile([P, Q], U32, name="q_codes", align_bytes=ALIGN)
         q_scales = sb.tile([P, Q], U8, name="q_scales", align_bytes=ALIGN)
-        o_codes = [sb.tile([P, w], U32, name="o_codes%d" % n, align_bytes=ALIGN) for n, (lo, w) in enumerate(CHUNKS)]
-        o_scales = [sb.tile([P, w], U8, name="o_scales%d" % n, align_bytes=ALIGN) for n, (lo, w) in enumerate(CHUNKS)]
+        o_grouped = [sb.tile([P, c[2], PACK], BF16, name="o_grouped%d" % n, align_bytes=ALIGN) for n, c in enumerate(CHUNKS)]
+        o_codes = [sb.tile([P, c[2]], U32, name="o_codes%d" % n, align_bytes=ALIGN) for n, c in enumerate(CHUNKS)]
+        o_scales = [sb.tile([P, c[2]], U8, name="o_scales%d" % n, align_bytes=ALIGN) for n, c in enumerate(CHUNKS)]
         b_ps = [ps.tile([P, BANK], F32, name="b_ps%d" % k) for k in range(len(BANKS))]
-        a_ps = ps.tile([P, I], F32, name="a_ps")
         rc_turned_ps = ps.tile([P, SLOT_TILES, P], F32, name="rc_turned_ps")
         rc_rows_ps = ps.tile([P, I], F32, name="rc_rows_ps")
-        o_grouped = {}
+        b_sb = sb.tile([P, U], F32, name="b_sb")
 
-        def cast(n, copy, tag):
-            o_grouped[n] = sb.tile([P, CHUNKS[n][1], PACK], BF16, name="o_grouped%d" % n, tag=tag, align_bytes=ALIGN)
-            interleave(copy, o_grouped[n], o_raw[n])
+        def cast(n):
+            load, lo, width, on_vector = CHUNKS[n]
+            at = lo - LOADS[load][0]
+            if on_vector > 0:
+                interleave(nc.vector.tensor_copy, o_grouped[n][:, :on_vector, :], o_raw[load][:, :, at : at + on_vector])
+            if on_vector < width:
+                interleave(nc.scalar.copy, o_grouped[n][:, on_vector:, :], o_raw[load][:, :, at + on_vector : at + width])
 
         def score_chunk(n):
-            lo, width = CHUNKS[n]
+            load, lo, width, on_vector = CHUNKS[n]
             in_bank = lo - BANKS[BANK_OF[n]][0]
             quantise(o_codes[n], o_scales[n], o_grouped[n])
             nc.tensor.matmul_mx(
@@ -129,51 +116,56 @@ def tile_attend_localscaling_kernel(tc, query, cand_words, cand_scales, other, r
             lo, hi = BANKS[k]
             nc.scalar.copy(b_sb[:, lo:hi], b_ps[k][:, : hi - lo])
 
-        listed_scales = sb.tile([P, I], U8, name="listed_scales", align_bytes=ALIGN)
-        nc.vector.tensor_copy(listed_scales[:], scales[:].indirect(offs_sb[:]))
-        interleave(nc.vector.tensor_copy, q_grouped, q_raw[:])
-        cast(1, nc.scalar.copy, "grouped1")
-        quantise(q_codes, q_scales, q_grouped)
-
-        listed_rc = sb.tile([P, I], F32, name="listed_rc", tag="scales", align_bytes=ALIGN)
+        listed_rc = sb.tile([P, I], F32, name="listed_rc", align_bytes=ALIGN)
         nc.vector.tensor_copy(listed_rc[:], rc_sb[:].indirect(offs_sb[:]))
         for c in range(SLOT_TILES):
             nc.tensor.transpose(rc_turned_ps[:, c, :], listed_rc[:, c * P : (c + 1) * P], ident[:])
+        listed_scale_rows = sb.tile([P, I], U8, name="listed_scale_rows", align_bytes=ALIGN)
+        nc.vector.tensor_copy(listed_scale_rows[:], scales[:].indirect(offs_sb[:]))
+        for quadrant in range(4):
+            nc.sync.dma_start(
+                listed_scales[32 * quadrant : 32 * quadrant + 4, :].bitcast(I32),
+                listed_scale_rows[SCALE_ROW + 4 * quadrant : SCALE_ROW + 4 * quadrant + 4, :].bitcast(I32),
+            )
+        interleave(nc.scalar.copy, q_grouped[:], q_raw[:])
+        quantise(q_codes, q_scales, q_grouped)
 
-        cast(0, nc.vector.tensor_copy, "rc_sb")
-        score_chunk(0)
-        score_chunk(1)
-        cast(2, nc.scalar.copy, "grouped2")
-        cast(3, nc.scalar.copy, "grouped3")
-        score_chunk(2)
-        cast(4, nc.vector.tensor_copy, "grouped2")
-        b_sb = sb.tile([P, U], F32, name="b_sb", tag="late_other")
-        empty_bank(0)
-        score_chunk(3)
-        score_chunk(4)
-        empty_bank(1)
-        empty_bank(2)
-
-        rc_repeated = sb.tile([P, SLOT_TILES, P], F32, name="rc_repeated", tag="grouped3", align_bytes=ALIGN)
-        nc.scalar.copy(rc_repeated[:], rc_turned_ps[:, :, 0:1].to_broadcast([P, SLOT_TILES, P]))
+        rc_repeated = sb.tile([P, SLOT_TILES, P], F32, name="rc_repeated", align_bytes=ALIGN)
+        nc.scalar.copy(rc_repeated[:], rc_turned_ps[:, :, RC_ROW:P].to_broadcast([P, SLOT_TILES, P]))
         for c in range(SLOT_TILES):
             nc.tensor.transpose(rc_rows_ps[:, c * P : (c + 1) * P], rc_repeated[:, c, :], ident[:])
 
-        listed_words = sb.tile([P, I], U16, name="listed_words", tag="grouped2", align_bytes=ALIGN)
-        nc.vector.tensor_copy(listed_words[:], words[:].indirect(offs_sb[:]))
-        nc.tensor.matmul_mx(
-            a_ps[:],
-            lhsT=q_codes[:].bitcast(FP8X4),
-            lhsT_scale=q_scales[:],
-            rhs=listed_words[:].bitcast(FP4X4),
-            rhs_scale=listed_scales[:],
-            start=True,
-            stop=True,
-        )
+        cast(0)
+        score_chunk(0)
+        cast(1)
+        cast(2)
+        empty_bank(0)
+        score_chunk(1)
+        score_chunk(2)
+        cast(3)
+        cast(4)
+        empty_bank(1)
+        score_chunk(3)
+        score_chunk(4)
+        empty_bank(2)
+        empty_bank(3)
+
+        a_ps = [ps.tile([P, BANK], F32, name="a_ps%d" % h, tag=tag) for h, tag in enumerate(("b_ps3", "a_ps1"))]
         halves = [slice(h * HALF, (h + 1) * HALF) for h in range(2)]
         twice_a = [sb.tile([P, HALF], F32, name="twice_a%d" % h) for h in range(2)]
         for h in range(2):
-            nc.scalar.activation(twice_a[h][:], a_ps[:, halves[h]], ACT.Copy, scale=2.0)
+            listed_words = sb.tile([P, HALF], U16, name="listed_words%d" % h, align_bytes=ALIGN)
+            nc.vector.tensor_copy(listed_words[:], words[:].indirect(offs_sb[:, h * HALF // 16 : (h + 1) * HALF // 16]))
+            nc.tensor.matmul_mx(
+                a_ps[h][:, :HALF],
+                lhsT=q_codes[:].bitcast(FP8X4),
+                lhsT_scale=q_scales[:],
+                rhs=listed_words[:].bitcast(FP4X4),
+                rhs_scale=listed_scales[:, halves[h]],
+                start=True,
+                stop=True,
+            )
+            nc.scalar.activation(twice_a[h][:], a_ps[h][:, :HALF], ACT.Copy, scale=2.0)
 
         listed_b = sb.tile([P, J], F32, name="listed_b")
         neg_mean = sb.tile([P, 1], F32, name="neg_mean")

@@ -26,10 +26,10 @@ ALIGN = 64
 SLOT_TILES = I // P
 HALF = I // 2
 
-LOADS = [(0, 256), (256, 384), (640, 256), (896, 128)]
-CHUNKS = [(0, 0, 256, 0), (1, 256, 256, 256), (1, 512, 128, 0), (2, 640, 256, 128), (3, 896, 128, 128)]
-BANKS = [(0, 256), (256, 640), (640, 896), (896, 1024)]
-BANK_OF = [0, 1, 1, 2, 3]
+LOADS = [(0, 512), (512, 384), (896, 128)]
+CHUNKS = [(0, 0, 256, 256), (0, 256, 256, 0), (1, 512, 256, 256), (1, 768, 128, 0), (2, 896, 128, 0)]
+BANKS = [(0, 512), (512, 896), (896, 1024)]
+BANK_OF = [0, 0, 1, 1, 2]
 RC_ROW = P - 1
 BLOCKS = D // 32
 SCALE_ROW = 48
@@ -39,6 +39,7 @@ def tile_attend_localscaling_kernel(tc, query, cand_words, cand_scales, other, r
     nc = tc.nc
     with ExitStack() as ctx:
         sb = ctx.enter_context(tc.tile_pool(name="sb", bufs=1))
+        late = ctx.enter_context(tc.tile_pool(name="late", bufs=1))
         ps = ctx.enter_context(tc.psum_pool(name="ps", bufs=1))
 
         def by_word(rows):
@@ -74,7 +75,10 @@ def tile_attend_localscaling_kernel(tc, query, cand_words, cand_scales, other, r
         nc.sync.dma_start(offs2_sb[:], offs2)
         o_raw = []
         for n, (lo, width) in enumerate(LOADS):
-            o_raw.append(sb.tile([P, PACK, width], F32, name="o_raw%d" % n))
+            if n < len(LOADS) - 1:
+                o_raw.append(sb.tile([P, PACK, width], F32, name="o_raw%d" % n))
+            else:
+                o_raw.append(late.tile([P, PACK, width], F32, name="o_raw%d" % n, offset=0))
             nc.sync.dma_start(o_raw[-1][:], by_word(other[:, lo : lo + width]))
         words = sb.tile([P, T], U16, name="words")
         nc.sync.dma_start(words[:].bitcast(I32), cand_words[0].bitcast(I32))
@@ -88,7 +92,10 @@ def tile_attend_localscaling_kernel(tc, query, cand_words, cand_scales, other, r
         b_ps = [ps.tile([P, BANK], F32, name="b_ps%d" % k) for k in range(len(BANKS))]
         rc_turned_ps = ps.tile([P, SLOT_TILES, P], F32, name="rc_turned_ps")
         rc_rows_ps = ps.tile([P, I], F32, name="rc_rows_ps")
-        b_sb = sb.tile([P, U], F32, name="b_sb")
+        listed_words = [
+            late.tile([P, HALF], U16, name="listed_words%d" % h, align_bytes=ALIGN, offset=2 * HALF * h) for h in range(2)
+        ]
+        b_sb = late.tile([P, U], F32, name="b_sb", offset=2 * I)
 
         def cast(n):
             load, lo, width, on_vector = CHUNKS[n]
@@ -136,45 +143,55 @@ def tile_attend_localscaling_kernel(tc, query, cand_words, cand_scales, other, r
             nc.tensor.transpose(rc_rows_ps[:, c * P : (c + 1) * P], rc_repeated[:, c, :], ident[:])
 
         cast(0)
-        score_chunk(0)
         cast(1)
-        cast(2)
-        empty_bank(0)
+        score_chunk(0)
         score_chunk(1)
-        score_chunk(2)
+        cast(2)
         cast(3)
         cast(4)
-        empty_bank(1)
+        empty_bank(0)
+        score_chunk(2)
         score_chunk(3)
         score_chunk(4)
+        empty_bank(1)
         empty_bank(2)
-        empty_bank(3)
 
-        a_ps = [ps.tile([P, BANK], F32, name="a_ps%d" % h, tag=tag) for h, tag in enumerate(("b_ps3", "a_ps1"))]
         halves = [slice(h * HALF, (h + 1) * HALF) for h in range(2)]
-        twice_a = [sb.tile([P, HALF], F32, name="twice_a%d" % h) for h in range(2)]
+        rc_rows = sb.tile([P, I], F32, name="rc_rows", tag="o_codes%d" % (len(CHUNKS) - 1), align_bytes=ALIGN)
         for h in range(2):
-            listed_words = sb.tile([P, HALF], U16, name="listed_words%d" % h, align_bytes=ALIGN)
-            nc.vector.tensor_copy(listed_words[:], words[:].indirect(offs_sb[:, h * HALF // 16 : (h + 1) * HALF // 16]))
+            nc.scalar.copy(rc_rows[:, halves[h]], rc_rows_ps[:, halves[h]])
+
+        a_ps = [ps.tile([P, BANK], F32, name="a_ps%d" % h) for h in range(2)]
+        for h in range(2):
+            nc.vector.tensor_copy(
+                listed_words[h][:], words[:].indirect(offs_sb[:, h * HALF // 16 : (h + 1) * HALF // 16])
+            )
             nc.tensor.matmul_mx(
                 a_ps[h][:, :HALF],
                 lhsT=q_codes[:].bitcast(FP8X4),
                 lhsT_scale=q_scales[:],
-                rhs=listed_words[:].bitcast(FP4X4),
+                rhs=listed_words[h][:].bitcast(FP4X4),
                 rhs_scale=listed_scales[:, halves[h]],
                 start=True,
                 stop=True,
             )
-            nc.scalar.activation(twice_a[h][:], a_ps[h][:, :HALF], ACT.Copy, scale=2.0)
 
-        listed_b = sb.tile([P, J], F32, name="listed_b")
-        neg_mean = sb.tile([P, 1], F32, name="neg_mean")
-        nc.vector.tensor_copy(listed_b[:], b_sb[:].indirect(offs2_sb[:]))
-        nc.vector.tensor_scalar(listed_b[:], listed_b[:], -1.0 / J, None, ALU.mult, ALU.add, accum_out=neg_mean[:])
+        means = []
+        for h in range(2):
+            listed_b = sb.tile([P, J // 2], F32, name="listed_b%d" % h)
+            scaled_b = sb.tile([P, J // 2], F32, name="scaled_b%d" % h)
+            means.append(sb.tile([P, 1], F32, name="mean%d" % h))
+            nc.vector.tensor_copy(listed_b[:], b_sb[:].indirect(offs2_sb[:, h * J // 32 : (h + 1) * J // 32]))
+            nc.scalar.activation(scaled_b[:], listed_b[:], ACT.Copy, scale=1.0 / J, accum_out=means[h][:])
 
+        without_mean = [sb.tile([P, HALF], F32, name="without_mean%d" % h) for h in range(2)]
+        for h in range(2):
+            nc.vector.scalar_tensor_tensor(
+                without_mean[h][:], a_ps[h][:, :HALF], 2.0, rc_rows[:, halves[h]], ALU.mult, ALU.subtract
+            )
         for h in range(2):
             result = sb.tile([P, HALF], F32, name="result%d" % h)
-            nc.vector.scalar_tensor_tensor(
-                result[:], twice_a[h][:], neg_mean[:], rc_rows_ps[:, halves[h]], ALU.add, ALU.subtract
+            nc.vector.tensor_scalar(
+                result[:], without_mean[h][:], means[0][:], means[1][:], ALU.subtract, ALU.subtract
             )
             nc.sync.dma_start(out[:, halves[h]], result[:])

@@ -26,10 +26,10 @@ ALIGN = 64
 SLOT_TILES = I // P
 HALF = I // 2
 
-LOADS = [(0, 512), (512, 384), (896, 128)]
-CHUNKS = [(0, 0, 256, 256), (0, 256, 256, 0), (1, 512, 256, 256), (1, 768, 128, 0), (2, 896, 128, 0)]
-BANKS = [(0, 512), (512, 896), (896, 1024)]
-BANK_OF = [0, 0, 1, 1, 2]
+LOADS = [(0, 512), (512, 256), (768, 256)]
+CHUNKS = [(0, 0, 256, 256), (0, 256, 256, 0), (1, 512, 256, 128), (2, 768, 128, 128), (2, 896, 128, 0)]
+BANKS = [(0, 512), (512, 768), (768, 896), (896, 1024)]
+BANK_OF = [0, 0, 1, 2, 3]
 RC_ROW = P - 1
 BLOCKS = D // 32
 SCALE_ROW = 48
@@ -72,7 +72,6 @@ def tile_attend_localscaling_kernel(tc, query, cand_words, cand_scales, other, r
         nc.sync.dma_start(rc_sb[RC_ROW:P, :], rc[0:1, :])
         nc.sync.dma_start(scales[SCALE_ROW : SCALE_ROW + BLOCKS, :].bitcast(I32), cand_scales[0].bitcast(I32))
         nc.sync.dma_start(q_raw[:], by_word(query))
-        nc.sync.dma_start(offs2_sb[:], offs2)
         o_raw = []
         for n, (lo, width) in enumerate(LOADS):
             if n < len(LOADS) - 1:
@@ -82,6 +81,7 @@ def tile_attend_localscaling_kernel(tc, query, cand_words, cand_scales, other, r
             nc.sync.dma_start(o_raw[-1][:], by_word(other[:, lo : lo + width]))
         words = sb.tile([P, T], U16, name="words")
         nc.sync.dma_start(words[:].bitcast(I32), cand_words[0].bitcast(I32))
+        nc.sync.dma_start(offs2_sb[:], offs2)
 
         q_grouped = sb.tile([P, Q, PACK], BF16, name="q_grouped", align_bytes=ALIGN)
         q_codes = sb.tile([P, Q], U32, name="q_codes", align_bytes=ALIGN)
@@ -145,16 +145,15 @@ def tile_attend_localscaling_kernel(tc, query, cand_words, cand_scales, other, r
         cast(0)
         cast(1)
         score_chunk(0)
-        score_chunk(1)
         cast(2)
+        score_chunk(1)
+        score_chunk(2)
         cast(3)
         cast(4)
-        empty_bank(0)
-        score_chunk(2)
         score_chunk(3)
         score_chunk(4)
-        empty_bank(1)
-        empty_bank(2)
+        for k in range(len(BANKS)):
+            empty_bank(k)
 
         halves = [slice(h * HALF, (h + 1) * HALF) for h in range(2)]
         rc_rows = sb.tile([P, I], F32, name="rc_rows", tag="o_codes%d" % (len(CHUNKS) - 1), align_bytes=ALIGN)

@@ -26,8 +26,8 @@ ALIGN = 64
 SLOT_TILES = I // P
 HALF = I // 2
 
-LOADS = [(0, 512), (512, 256), (768, 256)]
-CHUNKS = [(0, 0, 256, 256), (0, 256, 256, 0), (1, 512, 256, 128), (2, 768, 128, 128), (2, 896, 128, 0)]
+LOADS = [(0, 256), (256, 256), (512, 256), (768, 256)]
+CHUNKS = [(0, 0, 256, 0), (1, 256, 256, 0), (2, 512, 256, 128), (3, 768, 128, 128), (3, 896, 128, 0)]
 BANKS = [(0, 512), (512, 768), (768, 896), (896, 1024)]
 BANK_OF = [0, 0, 1, 2, 3]
 RC_ROW = P - 1
@@ -137,14 +137,15 @@ def tile_attend_localscaling_kernel(tc, query, cand_words, cand_scales, other, r
         interleave(nc.scalar.copy, q_grouped[:], q_raw[:])
         quantise(q_codes, q_scales, q_grouped)
 
-        rc_repeated = sb.tile([P, SLOT_TILES, P], F32, name="rc_repeated", align_bytes=ALIGN)
-        nc.scalar.copy(rc_repeated[:], rc_turned_ps[:, :, RC_ROW:P].to_broadcast([P, SLOT_TILES, P]))
-        for c in range(SLOT_TILES):
-            nc.tensor.transpose(rc_rows_ps[:, c * P : (c + 1) * P], rc_repeated[:, c, :], ident[:])
-
         cast(0)
-        cast(1)
+
+        rc_columns = sb.tile([P, SLOT_TILES], F32, name="rc_columns", tag="o_raw0")
+        nc.scalar.copy(rc_columns[:], rc_turned_ps[:, :, RC_ROW])
+        for c in range(SLOT_TILES):
+            nc.tensor.transpose(rc_rows_ps[:, c * P : (c + 1) * P], rc_columns[:, c : c + 1].to_broadcast([P, P]), ident[:])
+
         score_chunk(0)
+        cast(1)
         cast(2)
         score_chunk(1)
         score_chunk(2)

@@ -68,10 +68,10 @@ def tile_attend_localscaling_kernel(tc, query, cand_words, cand_scales, other, r
         listed_scales = sb.tile([P, I], U8, name="listed_scales", align_bytes=ALIGN)
         nc.gpsimd.memset(listed_scales[:].bitcast(I32), 0)
 
-        nc.sync.dma_start(offs_sb[:], offs)
         nc.sync.dma_start(rc_sb[RC_ROW:P, :], rc[0:1, :])
-        nc.sync.dma_start(scales[SCALE_ROW : SCALE_ROW + BLOCKS, :].bitcast(I32), cand_scales[0].bitcast(I32))
         nc.sync.dma_start(q_raw[:], by_word(query))
+        nc.sync.dma_start(offs_sb[:], offs)
+        nc.sync.dma_start(scales[SCALE_ROW : SCALE_ROW + BLOCKS, :].bitcast(I32), cand_scales[0].bitcast(I32))
         o_raw = []
         for n, (lo, width) in enumerate(LOADS):
             if n < len(LOADS) - 1:

@@ -27,9 +27,8 @@ SLOT_TILES = I // P
 HALF = I // 2
 
 LOADS = [(0, 256), (256, 256), (512, 256), (768, 256)]
-CHUNKS = [(0, 0, 256, 0), (1, 256, 256, 0), (2, 512, 256, 128), (3, 768, 128, 128), (3, 896, 128, 0)]
-BANKS = [(0, 512), (512, 768), (768, 896), (896, 1024)]
-BANK_OF = [0, 0, 1, 2, 3]
+CHUNKS = [(0, 0, 256, 0), (1, 256, 256, 128), (2, 512, 256, 128), (3, 768, 128, 128), (3, 896, 128, 0)]
+BANK_TAGS = ["bank0", "bank1", "bank3", "bank4", "bank2"]
 RC_ROW = P - 1
 BLOCKS = D // 32
 SCALE_ROW = 48
@@ -52,7 +51,7 @@ def tile_attend_localscaling_kernel(tc, query, cand_words, cand_scales, other, r
             )
 
         def quantise(codes, code_scales, grouped):
-            nc.vector.quantize_mx(codes[:].bitcast(FP8X4), code_scales[:], grouped[:].rearrange("p c t -> p (c t)"))
+            nc.vector.quantize_mx(codes[:].bitcast(FP8X4), code_scales[:], grouped.rearrange("p c t -> p (c t)"))
 
         offs_sb = sb.tile([P, I // 16], U16, name="offs_sb")
         offs2_sb = sb.tile([P, J // 16], U16, name="offs2_sb")
@@ -63,15 +62,19 @@ def tile_attend_localscaling_kernel(tc, query, cand_words, cand_scales, other, r
         nc.vector.memset(rc_sb[0:RC_ROW, :].bitcast(I32), 0)
         nc.gpsimd.memset(scales[0:SCALE_ROW, :].bitcast(I32), 0)
         nc.gpsimd.memset(scales[SCALE_ROW + BLOCKS : P, :].bitcast(I32), 0)
+        first_turn = late.tile([P, P], F32, name="first_turn", align_bytes=ALIGN, offset=8192 + 2048)
+        listed_rc = sb.tile([P, I], F32, name="listed_rc", align_bytes=ALIGN)
+        first_ident = first_turn[:, 0:P]
+        make_identity(nc, first_ident)
         ident = sb.tile([P, P], F32, name="ident")
         make_identity(nc, ident[:])
         listed_scales = sb.tile([P, I], U8, name="listed_scales", align_bytes=ALIGN)
         nc.gpsimd.memset(listed_scales[:].bitcast(I32), 0)
 
-        nc.sync.dma_start(rc_sb[RC_ROW:P, :], rc[0:1, :])
+        nc.scalar.dma_start(rc_sb[RC_ROW:P, :], rc[0:1, :])
         nc.sync.dma_start(q_raw[:], by_word(query))
         nc.sync.dma_start(offs_sb[:], offs)
-        nc.sync.dma_start(scales[SCALE_ROW : SCALE_ROW + BLOCKS, :].bitcast(I32), cand_scales[0].bitcast(I32))
+        nc.scalar.dma_start(scales[SCALE_ROW : SCALE_ROW + BLOCKS, :].bitcast(I32), cand_scales[0].bitcast(I32))
         o_raw = []
         for n, (lo, width) in enumerate(LOADS):
             if n < len(LOADS) - 1:
@@ -86,16 +89,21 @@ def tile_attend_localscaling_kernel(tc, query, cand_words, cand_scales, other, r
         q_grouped = sb.tile([P, Q, PACK], BF16, name="q_grouped", align_bytes=ALIGN)
         q_codes = sb.tile([P, Q], U32, name="q_codes", align_bytes=ALIGN)
         q_scales = sb.tile([P, Q], U8, name="q_scales", align_bytes=ALIGN)
-        o_grouped = [sb.tile([P, c[2], PACK], BF16, name="o_grouped%d" % n, align_bytes=ALIGN) for n, c in enumerate(CHUNKS)]
+        grouped_at = [0, 2304, 256, 256, 3328]
+        o_grouped = [
+            late.tile([P, c[2], PACK], BF16, name="o_grouped%d" % n, align_bytes=ALIGN, offset=8192 + grouped_at[n])[:]
+            for n, c in enumerate(CHUNKS)
+        ]
         o_codes = [sb.tile([P, c[2]], U32, name="o_codes%d" % n, align_bytes=ALIGN) for n, c in enumerate(CHUNKS)]
         o_scales = [sb.tile([P, c[2]], U8, name="o_scales%d" % n, align_bytes=ALIGN) for n, c in enumerate(CHUNKS)]
-        b_ps = [ps.tile([P, BANK], F32, name="b_ps%d" % k) for k in range(len(BANKS))]
-        rc_turned_ps = ps.tile([P, SLOT_TILES, P], F32, name="rc_turned_ps")
+        rc_turned_ps = ps.tile([P, SLOT_TILES, P], F32, name="rc_turned_ps", tag="bank0")
+        o_scales[2] = late.tile([P, 256], U8, name="held_scales", align_bytes=ALIGN, offset=8192 + 2304)
+        b_ps = [ps.tile([P, BANK], F32, name="b_ps%d" % n, tag=tag) for n, tag in enumerate(BANK_TAGS)]
         rc_rows_ps = ps.tile([P, I], F32, name="rc_rows_ps")
         listed_words = [
             late.tile([P, HALF], U16, name="listed_words%d" % h, align_bytes=ALIGN, offset=2 * HALF * h) for h in range(2)
         ]
-        b_sb = late.tile([P, U], F32, name="b_sb", offset=2 * I)
+        b_sb = sb.tile([P, U], F32, name="b_sb")
 
         def cast(n):
             load, lo, width, on_vector = CHUNKS[n]
@@ -107,10 +115,9 @@ def tile_attend_localscaling_kernel(tc, query, cand_words, cand_scales, other, r
 
         def score_chunk(n):
             load, lo, width, on_vector = CHUNKS[n]
-            in_bank = lo - BANKS[BANK_OF[n]][0]
             quantise(o_codes[n], o_scales[n], o_grouped[n])
             nc.tensor.matmul_mx(
-                b_ps[BANK_OF[n]][:, in_bank : in_bank + width],
+                b_ps[n][:, :width],
                 lhsT=q_codes[:].bitcast(FP8X4),
                 lhsT_scale=q_scales[:],
                 rhs=o_codes[n][:].bitcast(FP8X4),
@@ -119,14 +126,13 @@ def tile_attend_localscaling_kernel(tc, query, cand_words, cand_scales, other, r
                 stop=True,
             )
 
-        def empty_bank(k):
-            lo, hi = BANKS[k]
-            nc.scalar.copy(b_sb[:, lo:hi], b_ps[k][:, : hi - lo])
+        def empty_bank(n):
+            load, lo, width, on_vector = CHUNKS[n]
+            nc.scalar.copy(b_sb[:, lo : lo + width], b_ps[n][:, :width])
 
-        listed_rc = sb.tile([P, I], F32, name="listed_rc", align_bytes=ALIGN)
         nc.vector.tensor_copy(listed_rc[:], rc_sb[:].indirect(offs_sb[:]))
         for c in range(SLOT_TILES):
-            nc.tensor.transpose(rc_turned_ps[:, c, :], listed_rc[:, c * P : (c + 1) * P], ident[:])
+            nc.tensor.transpose(rc_turned_ps[:, c, :], listed_rc[:, c * P : (c + 1) * P], first_ident)
         listed_scale_rows = sb.tile([P, I], U8, name="listed_scale_rows", align_bytes=ALIGN)
         nc.vector.tensor_copy(listed_scale_rows[:], scales[:].indirect(offs_sb[:]))
         for quadrant in range(4):
@@ -135,26 +141,28 @@ def tile_attend_localscaling_kernel(tc, query, cand_words, cand_scales, other, r
                 listed_scale_rows[SCALE_ROW + 4 * quadrant : SCALE_ROW + 4 * quadrant + 4, :].bitcast(I32),
             )
         interleave(nc.scalar.copy, q_grouped[:], q_raw[:])
-        quantise(q_codes, q_scales, q_grouped)
+        quantise(q_codes, q_scales, q_grouped[:])
 
         cast(0)
 
-        rc_columns = sb.tile([P, SLOT_TILES], F32, name="rc_columns", tag="o_raw0")
+        rc_columns = sb.tile([P, SLOT_TILES], F32, name="rc_columns")
         nc.scalar.copy(rc_columns[:], rc_turned_ps[:, :, RC_ROW])
+        score_chunk(0)
         for c in range(SLOT_TILES):
             nc.tensor.transpose(rc_rows_ps[:, c * P : (c + 1) * P], rc_columns[:, c : c + 1].to_broadcast([P, P]), ident[:])
 
-        score_chunk(0)
         cast(1)
         cast(2)
+        empty_bank(0)
         score_chunk(1)
         score_chunk(2)
         cast(3)
         cast(4)
-        score_chunk(3)
-        score_chunk(4)
-        for k in range(len(BANKS)):
-            empty_bank(k)
+        empty_bank(1)
+        empty_bank(2)
+        for n in range(3, 5):
+            score_chunk(n)
+            empty_bank(n)
 
         halves = [slice(h * HALF, (h + 1) * HALF) for h in range(2)]
         rc_rows = sb.tile([P, I], F32, name="rc_rows", tag="o_codes%d" % (len(CHUNKS) - 1), align_bytes=ALIGN)

@@ -26,9 +26,20 @@ ALIGN = 64
 SLOT_TILES = I // P
 HALF = I // 2
 
-LOADS = [(0, 256), (256, 256), (512, 256), (768, 256)]
-CHUNKS = [(0, 0, 256, 0), (1, 256, 256, 128), (2, 512, 256, 128), (3, 768, 128, 128), (3, 896, 128, 0)]
-BANK_TAGS = ["bank0", "bank1", "bank3", "bank4", "bank2"]
+QUADRANT = 32
+
+LOADS = 4
+LOAD_WIDTH = U // LOADS
+CHUNKS = [(0, 256, 0), (256, 256, 128), (512, 256, 128), (768, 128, 128), (896, 128, 0)]
+LAST_CHUNK = len(CHUNKS) - 1
+
+GROUPED_BYTES = 2 * PACK * LOAD_WIDTH
+IDENT_BYTES = 4 * P
+CHUNK0_AT = 2 * 4 * PACK * LOAD_WIDTH
+IDENT_AT = CHUNK0_AT + GROUPED_BYTES
+CHUNK1_AT = IDENT_AT + IDENT_BYTES // 2
+CHUNK2_AT = CHUNK1_AT - GROUPED_BYTES
+GROUPED_AT = [CHUNK0_AT, CHUNK1_AT, CHUNK2_AT, CHUNK2_AT, CHUNK1_AT + GROUPED_BYTES // 2]
 RC_ROW = P - 1
 BLOCKS = D // 32
 SCALE_ROW = 48
@@ -38,7 +49,7 @@ def tile_attend_localscaling_kernel(tc, query, cand_words, cand_scales, other, r
     nc = tc.nc
     with ExitStack() as ctx:
         sb = ctx.enter_context(tc.tile_pool(name="sb", bufs=1))
-        late = ctx.enter_context(tc.tile_pool(name="late", bufs=1))
+        shared = ctx.enter_context(tc.tile_pool(name="shared", bufs=1))
         ps = ctx.enter_context(tc.psum_pool(name="ps", bufs=1))
 
         def by_word(rows):
@@ -51,7 +62,7 @@ def tile_attend_localscaling_kernel(tc, query, cand_words, cand_scales, other, r
             )
 
         def quantise(codes, code_scales, grouped):
-            nc.vector.quantize_mx(codes[:].bitcast(FP8X4), code_scales[:], grouped.rearrange("p c t -> p (c t)"))
+            nc.vector.quantize_mx(codes[:].bitcast(FP8X4), code_scales[:], grouped[:].rearrange("p c t -> p (c t)"))
 
         offs_sb = sb.tile([P, I // 16], U16, name="offs_sb")
         offs2_sb = sb.tile([P, J // 16], U16, name="offs2_sb")
@@ -62,12 +73,10 @@ def tile_attend_localscaling_kernel(tc, query, cand_words, cand_scales, other, r
         nc.vector.memset(rc_sb[0:RC_ROW, :].bitcast(I32), 0)
         nc.gpsimd.memset(scales[0:SCALE_ROW, :].bitcast(I32), 0)
         nc.gpsimd.memset(scales[SCALE_ROW + BLOCKS : P, :].bitcast(I32), 0)
-        first_turn = late.tile([P, P], F32, name="first_turn", align_bytes=ALIGN, offset=8192 + 2048)
-        listed_rc = sb.tile([P, I], F32, name="listed_rc", align_bytes=ALIGN)
-        first_ident = first_turn[:, 0:P]
-        make_identity(nc, first_ident)
-        ident = sb.tile([P, P], F32, name="ident")
-        make_identity(nc, ident[:])
+        first_ident = shared.tile([P, P], F32, name="first_ident", align_bytes=ALIGN, offset=IDENT_AT)
+        make_identity(nc, first_ident[:])
+        second_ident = sb.tile([P, P], F32, name="second_ident")
+        make_identity(nc, second_ident[:])
         listed_scales = sb.tile([P, I], U8, name="listed_scales", align_bytes=ALIGN)
         nc.gpsimd.memset(listed_scales[:].bitcast(I32), 0)
 
@@ -75,13 +84,10 @@ def tile_attend_localscaling_kernel(tc, query, cand_words, cand_scales, other, r
         nc.sync.dma_start(q_raw[:], by_word(query))
         nc.sync.dma_start(offs_sb[:], offs)
         nc.scalar.dma_start(scales[SCALE_ROW : SCALE_ROW + BLOCKS, :].bitcast(I32), cand_scales[0].bitcast(I32))
-        o_raw = []
-        for n, (lo, width) in enumerate(LOADS):
-            if n < len(LOADS) - 1:
-                o_raw.append(sb.tile([P, PACK, width], F32, name="o_raw%d" % n))
-            else:
-                o_raw.append(late.tile([P, PACK, width], F32, name="o_raw%d" % n, offset=0))
-            nc.sync.dma_start(o_raw[-1][:], by_word(other[:, lo : lo + width]))
+        o_raw = [sb.tile([P, PACK, LOAD_WIDTH], F32, name="o_raw%d" % n) for n in range(LOADS - 1)]
+        o_raw.append(shared.tile([P, PACK, LOAD_WIDTH], F32, name="o_raw_last", offset=0))
+        for n in range(LOADS):
+            nc.sync.dma_start(o_raw[n][:], by_word(other[:, n * LOAD_WIDTH : (n + 1) * LOAD_WIDTH]))
         words = sb.tile([P, T], U16, name="words")
         nc.sync.dma_start(words[:].bitcast(I32), cand_words[0].bitcast(I32))
         nc.sync.dma_start(offs2_sb[:], offs2)
@@ -89,32 +95,35 @@ def tile_attend_localscaling_kernel(tc, query, cand_words, cand_scales, other, r
         q_grouped = sb.tile([P, Q, PACK], BF16, name="q_grouped", align_bytes=ALIGN)
         q_codes = sb.tile([P, Q], U32, name="q_codes", align_bytes=ALIGN)
         q_scales = sb.tile([P, Q], U8, name="q_scales", align_bytes=ALIGN)
-        grouped_at = [0, 2304, 256, 256, 3328]
-        o_grouped = [
-            late.tile([P, c[2], PACK], BF16, name="o_grouped%d" % n, align_bytes=ALIGN, offset=8192 + grouped_at[n])[:]
-            for n, c in enumerate(CHUNKS)
-        ]
-        o_codes = [sb.tile([P, c[2]], U32, name="o_codes%d" % n, align_bytes=ALIGN) for n, c in enumerate(CHUNKS)]
-        o_scales = [sb.tile([P, c[2]], U8, name="o_scales%d" % n, align_bytes=ALIGN) for n, c in enumerate(CHUNKS)]
-        rc_turned_ps = ps.tile([P, SLOT_TILES, P], F32, name="rc_turned_ps", tag="bank0")
-        o_scales[2] = late.tile([P, 256], U8, name="held_scales", align_bytes=ALIGN, offset=8192 + 2304)
-        b_ps = [ps.tile([P, BANK], F32, name="b_ps%d" % n, tag=tag) for n, tag in enumerate(BANK_TAGS)]
+        o_grouped, o_codes, o_scales = [], [], []
+        for n, (lo, width, on_vector) in enumerate(CHUNKS):
+            o_grouped.append(
+                shared.tile([P, width, PACK], BF16, name="o_grouped%d" % n, align_bytes=ALIGN, offset=GROUPED_AT[n])
+            )
+            o_codes.append(sb.tile([P, width], U32, name="o_codes%d" % n, align_bytes=ALIGN))
+            if GROUPED_AT[n] == CHUNK2_AT and width == LOAD_WIDTH:
+                o_scales.append(shared.tile([P, width], U8, name="o_scales%d" % n, align_bytes=ALIGN, offset=CHUNK1_AT))
+            else:
+                o_scales.append(sb.tile([P, width], U8, name="o_scales%d" % n, align_bytes=ALIGN))
+        rc_turned_ps = ps.tile([P, SLOT_TILES, P], F32, name="rc_turned_ps", tag="b_ps0")
+        b_ps = [ps.tile([P, BANK], F32, name="b_ps%d" % n) for n in range(len(CHUNKS))]
         rc_rows_ps = ps.tile([P, I], F32, name="rc_rows_ps")
         listed_words = [
-            late.tile([P, HALF], U16, name="listed_words%d" % h, align_bytes=ALIGN, offset=2 * HALF * h) for h in range(2)
+            shared.tile([P, HALF], U16, name="listed_words%d" % h, align_bytes=ALIGN, offset=2 * HALF * h)
+            for h in range(2)
         ]
         b_sb = sb.tile([P, U], F32, name="b_sb")
 
         def cast(n):
-            load, lo, width, on_vector = CHUNKS[n]
-            at = lo - LOADS[load][0]
+            lo, width, on_vector = CHUNKS[n]
+            load, at = divmod(lo, LOAD_WIDTH)
             if on_vector > 0:
                 interleave(nc.vector.tensor_copy, o_grouped[n][:, :on_vector, :], o_raw[load][:, :, at : at + on_vector])
             if on_vector < width:
                 interleave(nc.scalar.copy, o_grouped[n][:, on_vector:, :], o_raw[load][:, :, at + on_vector : at + width])
 
         def score_chunk(n):
-            load, lo, width, on_vector = CHUNKS[n]
+            width = CHUNKS[n][1]
             quantise(o_codes[n], o_scales[n], o_grouped[n])
             nc.tensor.matmul_mx(
                 b_ps[n][:, :width],
@@ -127,21 +136,22 @@ def tile_attend_localscaling_kernel(tc, query, cand_words, cand_scales, other, r
             )
 
         def empty_bank(n):
-            load, lo, width, on_vector = CHUNKS[n]
+            lo, width = CHUNKS[n][:2]
             nc.scalar.copy(b_sb[:, lo : lo + width], b_ps[n][:, :width])
 
+        listed_rc = sb.tile([P, I], F32, name="listed_rc", align_bytes=ALIGN)
         nc.vector.tensor_copy(listed_rc[:], rc_sb[:].indirect(offs_sb[:]))
         for c in range(SLOT_TILES):
-            nc.tensor.transpose(rc_turned_ps[:, c, :], listed_rc[:, c * P : (c + 1) * P], first_ident)
+            nc.tensor.transpose(rc_turned_ps[:, c, :], listed_rc[:, c * P : (c + 1) * P], first_ident[:])
         listed_scale_rows = sb.tile([P, I], U8, name="listed_scale_rows", align_bytes=ALIGN)
         nc.vector.tensor_copy(listed_scale_rows[:], scales[:].indirect(offs_sb[:]))
-        for quadrant in range(4):
+        for quadrant in range(P // QUADRANT):
             nc.sync.dma_start(
-                listed_scales[32 * quadrant : 32 * quadrant + 4, :].bitcast(I32),
+                listed_scales[QUADRANT * quadrant : QUADRANT * quadrant + 4, :].bitcast(I32),
                 listed_scale_rows[SCALE_ROW + 4 * quadrant : SCALE_ROW + 4 * quadrant + 4, :].bitcast(I32),
             )
         interleave(nc.scalar.copy, q_grouped[:], q_raw[:])
-        quantise(q_codes, q_scales, q_grouped[:])
+        quantise(q_codes, q_scales, q_grouped)
 
         cast(0)
 
@@ -149,7 +159,9 @@ def tile_attend_localscaling_kernel(tc, query, cand_words, cand_scales, other, r
         nc.scalar.copy(rc_columns[:], rc_turned_ps[:, :, RC_ROW])
         score_chunk(0)
         for c in range(SLOT_TILES):
-            nc.tensor.transpose(rc_rows_ps[:, c * P : (c + 1) * P], rc_columns[:, c : c + 1].to_broadcast([P, P]), ident[:])
+            nc.tensor.transpose(
+                rc_rows_ps[:, c * P : (c + 1) * P], rc_columns[:, c : c + 1].to_broadcast([P, P]), second_ident[:]
+            )
 
         cast(1)
         cast(2)
@@ -160,12 +172,12 @@ def tile_attend_localscaling_kernel(tc, query, cand_words, cand_scales, other, r
         cast(4)
         empty_bank(1)
         empty_bank(2)
-        for n in range(3, 5):
+        for n in (LAST_CHUNK - 1, LAST_CHUNK):
             score_chunk(n)
             empty_bank(n)
 
         halves = [slice(h * HALF, (h + 1) * HALF) for h in range(2)]
-        rc_rows = sb.tile([P, I], F32, name="rc_rows", tag="o_codes%d" % (len(CHUNKS) - 1), align_bytes=ALIGN)
+        rc_rows = sb.tile([P, I], F32, name="rc_rows", tag="o_codes%d" % LAST_CHUNK, align_bytes=ALIGN)
         for h in range(2):
             nc.scalar.copy(rc_rows[:, halves[h]], rc_rows_ps[:, halves[h]])
 

@@ -25,24 +25,20 @@ BANK = 512
 ALIGN = 64
 SLOT_TILES = I // P
 HALF = I // 2
-
 QUADRANT = 32
-
-LOADS = 4
-LOAD_WIDTH = U // LOADS
-CHUNKS = [(0, 256, 0), (256, 256, 128), (512, 256, 128), (768, 128, 128), (896, 128, 0)]
-LAST_CHUNK = len(CHUNKS) - 1
-
-GROUPED_BYTES = 2 * PACK * LOAD_WIDTH
-IDENT_BYTES = 4 * P
-CHUNK0_AT = 2 * 4 * PACK * LOAD_WIDTH
-IDENT_AT = CHUNK0_AT + GROUPED_BYTES
-CHUNK1_AT = IDENT_AT + IDENT_BYTES // 2
-CHUNK2_AT = CHUNK1_AT - GROUPED_BYTES
-GROUPED_AT = [CHUNK0_AT, CHUNK1_AT, CHUNK2_AT, CHUNK2_AT, CHUNK1_AT + GROUPED_BYTES // 2]
 RC_ROW = P - 1
 BLOCKS = D // 32
 SCALE_ROW = 48
+
+LOADS = [(256, 0, [256]), (256, 128, [256]), (256, 128, [256]), (256, 192, [128, 128])]
+RAW_BYTES = [4 * PACK * load[0] for load in LOADS]
+CAST_BYTES = [2 * PACK * load[0] for load in LOADS]
+IDENT_BYTES = 4 * P
+IDENT_AT = RAW_BYTES[0]
+RAW_AT = [0] + [IDENT_BYTES + sum(RAW_BYTES[:n]) for n in range(1, len(LOADS))]
+B_AT = RAW_AT[3] + RAW_BYTES[3] // 2
+CAST0_AT = B_AT + 4 * U
+CAST_AT = [CAST0_AT, IDENT_AT + IDENT_BYTES // 2 - CAST_BYTES[1], RAW_AT[1], RAW_AT[2]]
 
 
 def tile_attend_localscaling_kernel(tc, query, cand_words, cand_scales, other, rc, offs, offs2, out):
@@ -55,14 +51,14 @@ def tile_attend_localscaling_kernel(tc, query, cand_words, cand_scales, other, r
         def by_word(rows):
             return rows.rearrange("(p t) c -> p t c", t=PACK)
 
-        def interleave(copy, grouped, raw):
-            copy(
-                grouped.rearrange("p (c i) t -> p c t i", i=RUN),
-                raw.rearrange("p t (c i) -> p c t i", i=RUN),
-            )
+        def cast_view(grouped):
+            return grouped.rearrange("p (c i) t -> p c t i", i=RUN)
+
+        def raw_view(raw):
+            return raw.rearrange("p t (c i) -> p c t i", i=RUN)
 
         def quantise(codes, code_scales, grouped):
-            nc.vector.quantize_mx(codes[:].bitcast(FP8X4), code_scales[:], grouped[:].rearrange("p c t -> p (c t)"))
+            nc.vector.quantize_mx(codes.bitcast(FP8X4), code_scales, grouped.rearrange("p c t -> p (c t)"))
 
         offs_sb = sb.tile([P, I // 16], U16, name="offs_sb")
         offs2_sb = sb.tile([P, J // 16], U16, name="offs2_sb")
@@ -84,60 +80,65 @@ def tile_attend_localscaling_kernel(tc, query, cand_words, cand_scales, other, r
         nc.sync.dma_start(q_raw[:], by_word(query))
         nc.sync.dma_start(offs_sb[:], offs)
         nc.scalar.dma_start(scales[SCALE_ROW : SCALE_ROW + BLOCKS, :].bitcast(I32), cand_scales[0].bitcast(I32))
-        o_raw = [sb.tile([P, PACK, LOAD_WIDTH], F32, name="o_raw%d" % n) for n in range(LOADS - 1)]
-        o_raw.append(shared.tile([P, PACK, LOAD_WIDTH], F32, name="o_raw_last", offset=0))
-        for n in range(LOADS):
-            nc.sync.dma_start(o_raw[n][:], by_word(other[:, n * LOAD_WIDTH : (n + 1) * LOAD_WIDTH]))
+        o_raw, o_cast, chunks = [], [], []
+        first = 0
+        for n, (width, on_vector, parts) in enumerate(LOADS):
+            o_raw.append(shared.tile([P, PACK, width], F32, name="o_raw%d" % n, offset=RAW_AT[n]))
+            nc.sync.dma_start(o_raw[n][:], by_word(other[:, first : first + width]))
+            at = 0
+            for part in parts:
+                chunks.append((n, at, first + at, part))
+                at += part
+            first += width
         words = sb.tile([P, T], U16, name="words")
         nc.sync.dma_start(words[:].bitcast(I32), cand_words[0].bitcast(I32))
         nc.sync.dma_start(offs2_sb[:], offs2)
+        last_chunk = len(chunks) - 1
 
-        q_grouped = sb.tile([P, Q, PACK], BF16, name="q_grouped", align_bytes=ALIGN)
+        q_cast = sb.tile([P, Q, PACK], BF16, name="q_cast", align_bytes=ALIGN)
         q_codes = sb.tile([P, Q], U32, name="q_codes", align_bytes=ALIGN)
         q_scales = sb.tile([P, Q], U8, name="q_scales", align_bytes=ALIGN)
-        o_grouped, o_codes, o_scales = [], [], []
-        for n, (lo, width, on_vector) in enumerate(CHUNKS):
-            o_grouped.append(
-                shared.tile([P, width, PACK], BF16, name="o_grouped%d" % n, align_bytes=ALIGN, offset=GROUPED_AT[n])
+        for n, (width, on_vector, parts) in enumerate(LOADS):
+            o_cast.append(
+                shared.tile([P, width, PACK], BF16, name="o_cast%d" % n, align_bytes=ALIGN, offset=CAST_AT[n])
             )
-            o_codes.append(sb.tile([P, width], U32, name="o_codes%d" % n, align_bytes=ALIGN))
-            if GROUPED_AT[n] == CHUNK2_AT and width == LOAD_WIDTH:
-                o_scales.append(shared.tile([P, width], U8, name="o_scales%d" % n, align_bytes=ALIGN, offset=CHUNK1_AT))
-            else:
-                o_scales.append(sb.tile([P, width], U8, name="o_scales%d" % n, align_bytes=ALIGN))
+        o_codes = [sb.tile([P, c[3]], U32, name="o_codes%d" % k, align_bytes=ALIGN) for k, c in enumerate(chunks)]
+        o_scales = [sb.tile([P, c[3]], U8, name="o_scales%d" % k, align_bytes=ALIGN) for k, c in enumerate(chunks)]
         rc_turned_ps = ps.tile([P, SLOT_TILES, P], F32, name="rc_turned_ps", tag="b_ps0")
-        b_ps = [ps.tile([P, BANK], F32, name="b_ps%d" % n) for n in range(len(CHUNKS))]
+        b_ps = [ps.tile([P, BANK], F32, name="b_ps%d" % k) for k in range(len(chunks))]
         rc_rows_ps = ps.tile([P, I], F32, name="rc_rows_ps")
         listed_words = [
-            shared.tile([P, HALF], U16, name="listed_words%d" % h, align_bytes=ALIGN, offset=2 * HALF * h)
+            shared.tile([P, HALF], U16, name="listed_words%d" % h, align_bytes=ALIGN, offset=RAW_AT[3] + 2 * HALF * h)
             for h in range(2)
         ]
-        b_sb = sb.tile([P, U], F32, name="b_sb")
+        b_sb = shared.tile([P, U], F32, name="b_sb", align_bytes=ALIGN, offset=B_AT)
 
         def cast(n):
-            lo, width, on_vector = CHUNKS[n]
-            load, at = divmod(lo, LOAD_WIDTH)
+            width, on_vector, parts = LOADS[n]
             if on_vector > 0:
-                interleave(nc.vector.tensor_copy, o_grouped[n][:, :on_vector, :], o_raw[load][:, :, at : at + on_vector])
+                step = min(on_vector, parts[0])
+                for lo in range(0, on_vector, step):
+                    hi = min(lo + step, on_vector)
+                    nc.vector.tensor_copy(cast_view(o_cast[n][:, lo:hi, :]), raw_view(o_raw[n][:, :, lo:hi]))
             if on_vector < width:
-                interleave(nc.scalar.copy, o_grouped[n][:, on_vector:, :], o_raw[load][:, :, at + on_vector : at + width])
+                nc.scalar.copy(cast_view(o_cast[n][:, on_vector:, :]), raw_view(o_raw[n][:, :, on_vector:]))
 
-        def score_chunk(n):
-            width = CHUNKS[n][1]
-            quantise(o_codes[n], o_scales[n], o_grouped[n])
+        def score_chunk(k):
+            n, at, first, width = chunks[k]
+            quantise(o_codes[k][:], o_scales[k][:], o_cast[n][:, at : at + width, :])
             nc.tensor.matmul_mx(
-                b_ps[n][:, :width],
+                b_ps[k][:, :width],
                 lhsT=q_codes[:].bitcast(FP8X4),
                 lhsT_scale=q_scales[:],
-                rhs=o_codes[n][:].bitcast(FP8X4),
-                rhs_scale=o_scales[n][:],
+                rhs=o_codes[k][:].bitcast(FP8X4),
+                rhs_scale=o_scales[k][:],
                 start=True,
                 stop=True,
             )
 
-        def empty_bank(n):
-            lo, width = CHUNKS[n][:2]
-            nc.scalar.copy(b_sb[:, lo : lo + width], b_ps[n][:, :width])
+        def empty_bank(k):
+            n, at, first, width = chunks[k]
+            nc.scalar.copy(b_sb[:, first : first + width], b_ps[k][:, :width])
 
         listed_rc = sb.tile([P, I], F32, name="listed_rc", align_bytes=ALIGN)
         nc.vector.tensor_copy(listed_rc[:], rc_sb[:].indirect(offs_sb[:]))
@@ -150,11 +151,10 @@ def tile_attend_localscaling_kernel(tc, query, cand_words, cand_scales, other, r
                 listed_scales[QUADRANT * quadrant : QUADRANT * quadrant + 4, :].bitcast(I32),
                 listed_scale_rows[SCALE_ROW + 4 * quadrant : SCALE_ROW + 4 * quadrant + 4, :].bitcast(I32),
             )
-        interleave(nc.scalar.copy, q_grouped[:], q_raw[:])
-        quantise(q_codes, q_scales, q_grouped)
+        nc.scalar.copy(cast_view(q_cast[:]), raw_view(q_raw[:]))
+        quantise(q_codes[:], q_scales[:], q_cast[:])
 
         cast(0)
-
         rc_columns = sb.tile([P, SLOT_TILES], F32, name="rc_columns")
         nc.scalar.copy(rc_columns[:], rc_turned_ps[:, :, RC_ROW])
         score_chunk(0)
@@ -162,22 +162,18 @@ def tile_attend_localscaling_kernel(tc, query, cand_words, cand_scales, other, r
             nc.tensor.transpose(
                 rc_rows_ps[:, c * P : (c + 1) * P], rc_columns[:, c : c + 1].to_broadcast([P, P]), second_ident[:]
             )
-
         cast(1)
         cast(2)
-        empty_bank(0)
         score_chunk(1)
         score_chunk(2)
         cast(3)
-        cast(4)
-        empty_bank(1)
-        empty_bank(2)
-        for n in (LAST_CHUNK - 1, LAST_CHUNK):
-            score_chunk(n)
-            empty_bank(n)
+        score_chunk(3)
+        score_chunk(4)
+        for k in range(len(chunks)):
+            empty_bank(k)
 
         halves = [slice(h * HALF, (h + 1) * HALF) for h in range(2)]
-        rc_rows = sb.tile([P, I], F32, name="rc_rows", tag="o_codes%d" % LAST_CHUNK, align_bytes=ALIGN)
+        rc_rows = sb.tile([P, I], F32, name="rc_rows", tag="o_codes%d" % last_chunk, align_bytes=ALIGN)
         for h in range(2):
             nc.scalar.copy(rc_rows[:, halves[h]], rc_rows_ps[:, halves[h]])
 

@@ -30,15 +30,27 @@ RC_ROW = P - 1
 BLOCKS = D // 32
 SCALE_ROW = 48
 
-LOADS = [(256, 0, [256]), (256, 128, [256]), (256, 128, [256]), (256, 192, [128, 128])]
-RAW_BYTES = [4 * PACK * load[0] for load in LOADS]
-CAST_BYTES = [2 * PACK * load[0] for load in LOADS]
+LOADS = [256, 256, 256, 256]
+STAGES = [
+    [("scalar", 0, 256)],
+    [("vector", 256, 128), ("scalar", 384, 128)],
+    [("vector", 512, 128), ("scalar", 640, 128)],
+    [("vector", 768, 128), ("vector", 896, 64), ("scalar", 960, 64)],
+]
+CHUNKS = [(0, 256), (256, 256), (512, 256), (768, 128), (896, 128)]
+LAST_CHUNK = len(CHUNKS) - 1
+BANKS = [(0, 256), (256, 256), (512, 256), (768, 128), (896, 128)]
+LAST_BANK = len(BANKS) - 1
+STAGE_WIDTH = [sum(piece[2] for piece in stage) for stage in STAGES]
+STAGE_FIRST = [sum(STAGE_WIDTH[:n]) for n in range(len(STAGES))]
+LOAD_FIRST = [sum(LOADS[:n]) for n in range(len(LOADS))]
+RAW_BYTES = [4 * PACK * width for width in LOADS]
 IDENT_BYTES = 4 * P
 IDENT_AT = RAW_BYTES[0]
 RAW_AT = [0] + [IDENT_BYTES + sum(RAW_BYTES[:n]) for n in range(1, len(LOADS))]
-B_AT = RAW_AT[3] + RAW_BYTES[3] // 2
-CAST0_AT = B_AT + 4 * U
-CAST_AT = [CAST0_AT, IDENT_AT + IDENT_BYTES // 2 - CAST_BYTES[1], RAW_AT[1], RAW_AT[2]]
+B_AT = RAW_AT[1] + RAW_BYTES[1] // 2
+FREE_AT = max(RAW_AT[-1] + RAW_BYTES[-1], 2 * I + RAW_AT[-1])
+CAST_AT = [FREE_AT + 4 * U + 2 * HALF, IDENT_AT + IDENT_BYTES // 2 - 2 * PACK * STAGE_WIDTH[1], RAW_AT[1], RAW_AT[2] + RAW_BYTES[2] // 2]
 
 
 def tile_attend_localscaling_kernel(tc, query, cand_words, cand_scales, other, rc, offs, offs2, out):
@@ -80,54 +92,48 @@ def tile_attend_localscaling_kernel(tc, query, cand_words, cand_scales, other, r
         nc.sync.dma_start(q_raw[:], by_word(query))
         nc.sync.dma_start(offs_sb[:], offs)
         nc.scalar.dma_start(scales[SCALE_ROW : SCALE_ROW + BLOCKS, :].bitcast(I32), cand_scales[0].bitcast(I32))
-        o_raw, o_cast, chunks = [], [], []
-        first = 0
-        for n, (width, on_vector, parts) in enumerate(LOADS):
+        o_raw = []
+        for n, width in enumerate(LOADS):
             o_raw.append(shared.tile([P, PACK, width], F32, name="o_raw%d" % n, offset=RAW_AT[n]))
-            nc.sync.dma_start(o_raw[n][:], by_word(other[:, first : first + width]))
-            at = 0
-            for part in parts:
-                chunks.append((n, at, first + at, part))
-                at += part
-            first += width
+            nc.sync.dma_start(o_raw[n][:], by_word(other[:, LOAD_FIRST[n] : LOAD_FIRST[n] + width]))
         words = sb.tile([P, T], U16, name="words")
         nc.sync.dma_start(words[:].bitcast(I32), cand_words[0].bitcast(I32))
         nc.sync.dma_start(offs2_sb[:], offs2)
-        last_chunk = len(chunks) - 1
 
         q_cast = sb.tile([P, Q, PACK], BF16, name="q_cast", align_bytes=ALIGN)
         q_codes = sb.tile([P, Q], U32, name="q_codes", align_bytes=ALIGN)
         q_scales = sb.tile([P, Q], U8, name="q_scales", align_bytes=ALIGN)
-        for n, (width, on_vector, parts) in enumerate(LOADS):
-            o_cast.append(
-                shared.tile([P, width, PACK], BF16, name="o_cast%d" % n, align_bytes=ALIGN, offset=CAST_AT[n])
-            )
-        o_codes = [sb.tile([P, c[3]], U32, name="o_codes%d" % k, align_bytes=ALIGN) for k, c in enumerate(chunks)]
-        o_scales = [sb.tile([P, c[3]], U8, name="o_scales%d" % k, align_bytes=ALIGN) for k, c in enumerate(chunks)]
+        o_cast = [
+            shared.tile([P, width, PACK], BF16, name="o_cast%d" % n, align_bytes=ALIGN, offset=CAST_AT[n])
+            for n, width in enumerate(STAGE_WIDTH)
+        ]
+        o_codes = [sb.tile([P, c[1]], U32, name="o_codes%d" % k, align_bytes=ALIGN) for k, c in enumerate(CHUNKS)]
+        o_scales = [sb.tile([P, c[1]], U8, name="o_scales%d" % k, align_bytes=ALIGN) for k, c in enumerate(CHUNKS)]
         rc_turned_ps = ps.tile([P, SLOT_TILES, P], F32, name="rc_turned_ps", tag="b_ps0")
-        b_ps = [ps.tile([P, BANK], F32, name="b_ps%d" % k) for k in range(len(chunks))]
+        b_ps = [ps.tile([P, BANK], F32, name="b_ps%d" % k) for k in range(len(BANKS))]
         rc_rows_ps = ps.tile([P, I], F32, name="rc_rows_ps")
         listed_words = [
-            shared.tile([P, HALF], U16, name="listed_words%d" % h, align_bytes=ALIGN, offset=RAW_AT[3] + 2 * HALF * h)
-            for h in range(2)
+            shared.tile([P, HALF], U16, name="listed_words%d" % h, align_bytes=ALIGN, offset=at)
+            for h, at in enumerate([RAW_AT[-1], RAW_AT[-1] + 2 * HALF])
         ]
         b_sb = shared.tile([P, U], F32, name="b_sb", align_bytes=ALIGN, offset=B_AT)
 
-        def cast(n):
-            width, on_vector, parts = LOADS[n]
-            if on_vector > 0:
-                step = min(on_vector, parts[0])
-                for lo in range(0, on_vector, step):
-                    hi = min(lo + step, on_vector)
-                    nc.vector.tensor_copy(cast_view(o_cast[n][:, lo:hi, :]), raw_view(o_raw[n][:, :, lo:hi]))
-            if on_vector < width:
-                nc.scalar.copy(cast_view(o_cast[n][:, on_vector:, :]), raw_view(o_raw[n][:, :, on_vector:]))
+        def cast(stage):
+            for engine, first, width in STAGES[stage]:
+                load = max(n for n in range(len(LOADS)) if LOAD_FIRST[n] <= first)
+                at, to = first - LOAD_FIRST[load], first - STAGE_FIRST[stage]
+                copy = nc.vector.tensor_copy if engine == "vector" else nc.scalar.copy
+                copy(cast_view(o_cast[stage][:, to : to + width, :]), raw_view(o_raw[load][:, :, at : at + width]))
 
         def score_chunk(k):
-            n, at, first, width = chunks[k]
-            quantise(o_codes[k][:], o_scales[k][:], o_cast[n][:, at : at + width, :])
+            first, width = CHUNKS[k]
+            stage = max(n for n in range(len(STAGES)) if STAGE_FIRST[n] <= first)
+            at = first - STAGE_FIRST[stage]
+            quantise(o_codes[k][:], o_scales[k][:], o_cast[stage][:, at : at + width, :])
+            bank = max(n for n in range(len(BANKS)) if BANKS[n][0] <= first)
+            place = first - BANKS[bank][0]
             nc.tensor.matmul_mx(
-                b_ps[k][:, :width],
+                b_ps[bank][:, place : place + width],
                 lhsT=q_codes[:].bitcast(FP8X4),
                 lhsT_scale=q_scales[:],
                 rhs=o_codes[k][:].bitcast(FP8X4),
@@ -137,7 +143,7 @@ def tile_attend_localscaling_kernel(tc, query, cand_words, cand_scales, other, r
             )
 
         def empty_bank(k):
-            n, at, first, width = chunks[k]
+            first, width = BANKS[k]
             nc.scalar.copy(b_sb[:, first : first + width], b_ps[k][:, :width])
 
         listed_rc = sb.tile([P, I], F32, name="listed_rc", align_bytes=ALIGN)
@@ -164,16 +170,17 @@ def tile_attend_localscaling_kernel(tc, query, cand_words, cand_scales, other, r
             )
         cast(1)
         cast(2)
+        empty_bank(0)
         score_chunk(1)
         score_chunk(2)
         cast(3)
         score_chunk(3)
         score_chunk(4)
-        for k in range(len(chunks)):
+        for k in range(1, len(BANKS)):
             empty_bank(k)
 
         halves = [slice(h * HALF, (h + 1) * HALF) for h in range(2)]
-        rc_rows = sb.tile([P, I], F32, name="rc_rows", tag="o_codes%d" % last_chunk, align_bytes=ALIGN)
+        rc_rows = sb.tile([P, I], F32, name="rc_rows", tag="o_codes%d" % LAST_CHUNK, align_bytes=ALIGN)
         for h in range(2):
             nc.scalar.copy(rc_rows[:, halves[h]], rc_rows_ps[:, halves[h]])
 

@@ -33,7 +33,7 @@ SCALE_ROW = 48
 LOADS = [256, 256, 256, 256]
 STAGES = [
     [("scalar", 0, 256)],
-    [("vector", 256, 128), ("scalar", 384, 128)],
+    [("vector", 256, 64), ("scalar", 320, 192)],
     [("vector", 512, 128), ("scalar", 640, 128)],
     [("vector", 768, 128), ("vector", 896, 64), ("scalar", 960, 64)],
 ]
@@ -47,10 +47,10 @@ LOAD_FIRST = [sum(LOADS[:n]) for n in range(len(LOADS))]
 RAW_BYTES = [4 * PACK * width for width in LOADS]
 IDENT_BYTES = 4 * P
 IDENT_AT = RAW_BYTES[0]
-RAW_AT = [0] + [IDENT_BYTES + sum(RAW_BYTES[:n]) for n in range(1, len(LOADS))]
+RAW_AT = [0] + [IDENT_BYTES + 2 * PACK * STAGE_WIDTH[1] + sum(RAW_BYTES[:n]) for n in range(1, len(LOADS))]
 B_AT = RAW_AT[1] + RAW_BYTES[1] // 2
 FREE_AT = max(RAW_AT[-1] + RAW_BYTES[-1], 2 * I + RAW_AT[-1])
-CAST_AT = [FREE_AT + 4 * U + 2 * HALF, IDENT_AT + IDENT_BYTES // 2 - 2 * PACK * STAGE_WIDTH[1], RAW_AT[1], RAW_AT[2] + RAW_BYTES[2] // 2]
+CAST_AT = [FREE_AT + 4 * U + 2 * HALF, IDENT_AT + IDENT_BYTES // 2, IDENT_AT + IDENT_BYTES // 2 - 2 * PACK * STAGE_WIDTH[2], RAW_AT[2] + RAW_BYTES[2] // 2]
 
 
 def tile_attend_localscaling_kernel(tc, query, cand_words, cand_scales, other, rc, offs, offs2, out):

@@ -48,7 +48,7 @@ RAW_BYTES = [4 * PACK * width for width in LOADS]
 IDENT_BYTES = 4 * P
 IDENT_AT = RAW_BYTES[0]
 RAW_AT = [0] + [IDENT_BYTES + 2 * PACK * STAGE_WIDTH[1] + sum(RAW_BYTES[:n]) for n in range(1, len(LOADS))]
-B_AT = RAW_AT[1] + RAW_BYTES[1] // 2
+B_AT = RAW_AT[1]
 FREE_AT = max(RAW_AT[-1] + RAW_BYTES[-1], 2 * I + RAW_AT[-1])
 CAST_AT = [FREE_AT + 4 * U + 2 * HALF, IDENT_AT + IDENT_BYTES // 2, IDENT_AT + IDENT_BYTES // 2 - 2 * PACK * STAGE_WIDTH[2], RAW_AT[2] + RAW_BYTES[2] // 2]
 
@@ -174,16 +174,14 @@ def tile_attend_localscaling_kernel(tc, query, cand_words, cand_scales, other, r
         score_chunk(1)
         score_chunk(2)
         cast(3)
+        rc_rows = shared.tile([P, I], F32, name="rc_rows", align_bytes=ALIGN, offset=RAW_AT[2])
+        nc.scalar.copy(rc_rows[:], rc_rows_ps[:])
         score_chunk(3)
         score_chunk(4)
         for k in range(1, len(BANKS)):
             empty_bank(k)
 
         halves = [slice(h * HALF, (h + 1) * HALF) for h in range(2)]
-        rc_rows = sb.tile([P, I], F32, name="rc_rows", tag="o_codes%d" % LAST_CHUNK, align_bytes=ALIGN)
-        for h in range(2):
-            nc.scalar.copy(rc_rows[:, halves[h]], rc_rows_ps[:, halves[h]])
-
         a_ps = [ps.tile([P, BANK], F32, name="a_ps%d" % h) for h in range(2)]
         for h in range(2):
             nc.vector.tensor_copy(

@@ -30,6 +30,7 @@ RC_ROW = P - 1
 BLOCKS = D // 32
 SCALE_ROW = 48
 
+SCALAR_LOOKUPS = 64
 LOADS = [256, 256, 256, 256]
 STAGES = [
     [("scalar", 0, 256)],
@@ -197,13 +198,19 @@ def tile_attend_localscaling_kernel(tc, query, cand_words, cand_scales, other, r
                 stop=True,
             )
 
-        means = []
+        means = [sb.tile([P, 1], F32, name="mean%d" % h) for h in range(2)]
+        listed_b = [sb.tile([P, J // 2], F32, name="listed_b%d" % h) for h in range(2)]
+        scaled_b = [sb.tile([P, J // 2], F32, name="scaled_b%d" % h) for h in range(2)]
+        split = J // 2 - SCALAR_LOOKUPS
+        nc.scalar.activation(
+            listed_b[1][:, split:], b_sb[:].indirect(offs2_sb[:, (J - SCALAR_LOOKUPS) // 16 :]), ACT.Copy
+        )
+        nc.vector.tensor_copy(listed_b[0][:], b_sb[:].indirect(offs2_sb[:, : J // 32]))
+        nc.vector.tensor_copy(
+            listed_b[1][:, :split], b_sb[:].indirect(offs2_sb[:, J // 32 : (J - SCALAR_LOOKUPS) // 16])
+        )
         for h in range(2):
-            listed_b = sb.tile([P, J // 2], F32, name="listed_b%d" % h)
-            scaled_b = sb.tile([P, J // 2], F32, name="scaled_b%d" % h)
-            means.append(sb.tile([P, 1], F32, name="mean%d" % h))
-            nc.vector.tensor_copy(listed_b[:], b_sb[:].indirect(offs2_sb[:, h * J // 32 : (h + 1) * J // 32]))
-            nc.scalar.activation(scaled_b[:], listed_b[:], ACT.Copy, scale=1.0 / J, accum_out=means[h][:])
+            nc.scalar.activation(scaled_b[h][:], listed_b[h][:], ACT.Copy, scale=1.0 / J, accum_out=means[h][:])
 
         without_mean = [sb.tile([P, HALF], F32, name="without_mean%d" % h) for h in range(2)]
         for h in range(2):

@@ -30,12 +30,13 @@ RC_ROW = P - 1
 BLOCKS = D // 32
 SCALE_ROW = 48
 
-SCALAR_LOOKUPS = 64
+SCALAR_LOOKUPS = 96
+FIRST_LOOKUPS = 96
 LOADS = [256, 256, 256, 256]
 STAGES = [
     [("scalar", 0, 256)],
-    [("vector", 256, 64), ("scalar", 320, 192)],
-    [("vector", 512, 128), ("scalar", 640, 128)],
+    [("vector", 256, 96), ("scalar", 352, 160)],
+    [("vector", 512, 160), ("scalar", 672, 96)],
     [("vector", 768, 128), ("vector", 896, 64), ("scalar", 960, 64)],
 ]
 CHUNKS = [(0, 256), (256, 256), (512, 256), (768, 128), (896, 128)]
@@ -199,15 +200,16 @@ def tile_attend_localscaling_kernel(tc, query, cand_words, cand_scales, other, r
             )
 
         means = [sb.tile([P, 1], F32, name="mean%d" % h) for h in range(2)]
-        listed_b = [sb.tile([P, J // 2], F32, name="listed_b%d" % h) for h in range(2)]
-        scaled_b = [sb.tile([P, J // 2], F32, name="scaled_b%d" % h) for h in range(2)]
-        split = J // 2 - SCALAR_LOOKUPS
+        parts = [FIRST_LOOKUPS, J - FIRST_LOOKUPS]
+        listed_b = [sb.tile([P, parts[h]], F32, name="listed_b%d" % h) for h in range(2)]
+        scaled_b = [sb.tile([P, parts[h]], F32, name="scaled_b%d" % h) for h in range(2)]
+        split = parts[1] - SCALAR_LOOKUPS
         nc.scalar.activation(
             listed_b[1][:, split:], b_sb[:].indirect(offs2_sb[:, (J - SCALAR_LOOKUPS) // 16 :]), ACT.Copy
         )
-        nc.vector.tensor_copy(listed_b[0][:], b_sb[:].indirect(offs2_sb[:, : J // 32]))
+        nc.vector.tensor_copy(listed_b[0][:], b_sb[:].indirect(offs2_sb[:, : FIRST_LOOKUPS // 16]))
         nc.vector.tensor_copy(
-            listed_b[1][:, :split], b_sb[:].indirect(offs2_sb[:, J // 32 : (J - SCALAR_LOOKUPS) // 16])
+            listed_b[1][:, :split], b_sb[:].indirect(offs2_sb[:, FIRST_LOOKUPS // 16 : (J - SCALAR_LOOKUPS) // 16])
         )
         for h in range(2):
             nc.scalar.activation(scaled_b[h][:], listed_b[h][:], ACT.Copy, scale=1.0 / J, accum_out=means[h][:])

@@ -23,6 +23,7 @@ PACK = 4
 RUN = 4
 BANK = 512
 ALIGN = 64
+DMA_ALIGN = 256
 SLOT_TILES = I // P
 HALF = I // 2
 QUADRANT = 32
@@ -76,9 +77,9 @@ def tile_attend_localscaling_kernel(tc, query, cand_words, cand_scales, other, r
 
         offs_sb = sb.tile([P, I // 16], U16, name="offs_sb")
         offs2_sb = sb.tile([P, J // 16], U16, name="offs2_sb")
-        q_raw = sb.tile([P, PACK, Q], F32, name="q_raw")
-        scales = sb.tile([P, T], U8, name="scales", align_bytes=ALIGN)
-        rc_sb = sb.tile([P, T], F32, name="rc_sb", align_bytes=ALIGN)
+        q_raw = sb.tile([P, PACK, Q], F32, name="q_raw", align_bytes=DMA_ALIGN)
+        scales = sb.tile([P, T], U8, name="scales", align_bytes=DMA_ALIGN)
+        rc_sb = sb.tile([P, T], F32, name="rc_sb", align_bytes=DMA_ALIGN)
 
         nc.vector.memset(rc_sb[0:RC_ROW, :].bitcast(I32), 0)
         nc.gpsimd.memset(scales[0:SCALE_ROW, :].bitcast(I32), 0)
@@ -96,9 +97,9 @@ def tile_attend_localscaling_kernel(tc, query, cand_words, cand_scales, other, r
         nc.scalar.dma_start(scales[SCALE_ROW : SCALE_ROW + BLOCKS, :].bitcast(I32), cand_scales[0].bitcast(I32))
         o_raw = []
         for n, width in enumerate(LOADS):
-            o_raw.append(shared.tile([P, PACK, width], F32, name="o_raw%d" % n, offset=RAW_AT[n]))
+            o_raw.append(shared.tile([P, PACK, width], F32, name="o_raw%d" % n, align_bytes=DMA_ALIGN, offset=RAW_AT[n]))
             nc.sync.dma_start(o_raw[n][:], by_word(other[:, LOAD_FIRST[n] : LOAD_FIRST[n] + width]))
-        words = sb.tile([P, T], U16, name="words")
+        words = sb.tile([P, T], U16, name="words", align_bytes=DMA_ALIGN)
         nc.sync.dma_start(words[:].bitcast(I32), cand_words[0].bitcast(I32))
         nc.sync.dma_start(offs2_sb[:], offs2)
 
@@ -220,7 +221,7 @@ def tile_attend_localscaling_kernel(tc, query, cand_words, cand_scales, other, r
                 without_mean[h][:], a_ps[h][:, :HALF], 2.0, rc_rows[:, halves[h]], ALU.mult, ALU.subtract
             )
         for h in range(2):
-            result = sb.tile([P, HALF], F32, name="result%d" % h)
+            result = sb.tile([P, HALF], F32, name="result%d" % h, align_bytes=DMA_ALIGN)
             nc.vector.tensor_scalar(
                 result[:], without_mean[h][:], means[0][:], means[1][:], ALU.subtract, ALU.subtract
             )

@@ -23,7 +23,7 @@ PACK = 4
 RUN = 4
 BANK = 512
 ALIGN = 64
-DMA_ALIGN = 256
+DMA_ALIGN = 1024
 SLOT_TILES = I // P
 HALF = I // 2
 QUADRANT = 32
@@ -50,7 +50,7 @@ LOAD_FIRST = [sum(LOADS[:n]) for n in range(len(LOADS))]
 RAW_BYTES = [4 * PACK * width for width in LOADS]
 IDENT_BYTES = 4 * P
 IDENT_AT = RAW_BYTES[0]
-RAW_AT = [0] + [IDENT_BYTES + 2 * PACK * STAGE_WIDTH[1] + sum(RAW_BYTES[:n]) for n in range(1, len(LOADS))]
+RAW_AT = [0] + [DMA_ALIGN + 2 * PACK * STAGE_WIDTH[1] + sum(RAW_BYTES[:n]) for n in range(1, len(LOADS))]
 B_AT = RAW_AT[1]
 FREE_AT = max(RAW_AT[-1] + RAW_BYTES[-1], 2 * I + RAW_AT[-1])
 CAST_AT = [FREE_AT + 4 * U + 2 * HALF, IDENT_AT + IDENT_BYTES // 2, IDENT_AT + IDENT_BYTES // 2 - 2 * PACK * STAGE_WIDTH[2], RAW_AT[2] + RAW_BYTES[2] // 2]

from contextlib import ExitStack

import concourse.mybir as mybir
from concourse.masks import make_identity

D, T, I, U, J, Q = 512, 2048, 512, 1024, 256, 128
FLOPS = 2 * D * Q * (I + U)
BYTES = 4 * D * Q + 2 * 128 * T + 16 * T + 4 * D * U + 4 * T + 2 * 128 * (I + J) // 16 + 4 * Q * I

F32 = mybir.dt.float32
BF16 = mybir.dt.bfloat16
I32 = mybir.dt.int32
U32 = mybir.dt.uint32
U16 = mybir.dt.uint16
U8 = mybir.dt.uint8
FP8X4 = mybir.dt.float8_e4m3fn_x4
FP4X4 = mybir.dt.float4_e2m1fn_x4
ALU = mybir.AluOpType
ACT = mybir.ActivationFunctionType

P = 128
PACK = 4
RUN = 4
BANK = 512
ALIGN = 64
DMA_ALIGN = 1024
SLOT_TILES = I // P
HALF = I // 2
QUADRANT = 32
RC_ROW = P - 1
BLOCKS = D // 32
SCALE_ROW = 48

SCALAR_LOOKUPS = 96
FIRST_LOOKUPS = 96
LOADS = [256, 256, 256, 256]
STAGES = [
    [("scalar", 0, 256)],
    [("vector", 256, 96), ("scalar", 352, 160)],
    [("vector", 512, 160), ("scalar", 672, 96)],
    [("vector", 768, 128), ("vector", 896, 64), ("scalar", 960, 64)],
]
CHUNKS = [(0, 256), (256, 256), (512, 256), (768, 128), (896, 128)]
LAST_CHUNK = len(CHUNKS) - 1
BANKS = [(0, 256), (256, 256), (512, 256), (768, 128), (896, 128)]
LAST_BANK = len(BANKS) - 1
STAGE_WIDTH = [sum(piece[2] for piece in stage) for stage in STAGES]
STAGE_FIRST = [sum(STAGE_WIDTH[:n]) for n in range(len(STAGES))]
LOAD_FIRST = [sum(LOADS[:n]) for n in range(len(LOADS))]
RAW_BYTES = [4 * PACK * width for width in LOADS]
IDENT_BYTES = 4 * P
IDENT_AT = RAW_BYTES[0]
RAW_AT = [0] + [DMA_ALIGN + 2 * PACK * STAGE_WIDTH[1] + sum(RAW_BYTES[:n]) for n in range(1, len(LOADS))]
B_AT = RAW_AT[1]
FREE_AT = max(RAW_AT[-1] + RAW_BYTES[-1], 2 * I + RAW_AT[-1])
CAST_AT = [FREE_AT + 4 * U + 2 * HALF, IDENT_AT + IDENT_BYTES // 2, IDENT_AT + IDENT_BYTES // 2 - 2 * PACK * STAGE_WIDTH[2], RAW_AT[2] + RAW_BYTES[2] // 2]


def tile_attend_localscaling_kernel(tc, query, cand_words, cand_scales, other, rc, offs, offs2, out):
    nc = tc.nc
    with ExitStack() as ctx:
        sb = ctx.enter_context(tc.tile_pool(name="sb", bufs=1))
        shared = ctx.enter_context(tc.tile_pool(name="shared", bufs=1))
        ps = ctx.enter_context(tc.psum_pool(name="ps", bufs=1))

        def by_word(rows):
            return rows.rearrange("(p t) c -> p t c", t=PACK)

        def cast_view(grouped):
            return grouped.rearrange("p (c i) t -> p c t i", i=RUN)

        def raw_view(raw):
            return raw.rearrange("p t (c i) -> p c t i", i=RUN)

        def quantise(codes, code_scales, grouped):
            nc.vector.quantize_mx(codes.bitcast(FP8X4), code_scales, grouped.rearrange("p c t -> p (c t)"))

        offs_sb = sb.tile([P, I // 16], U16, name="offs_sb")
        offs2_sb = sb.tile([P, J // 16], U16, name="offs2_sb")
        q_raw = sb.tile([P, PACK, Q], F32, name="q_raw", align_bytes=DMA_ALIGN)
        scales = sb.tile([P, T], U8, name="scales", align_bytes=DMA_ALIGN)
        rc_sb = sb.tile([P, T], F32, name="rc_sb", align_bytes=DMA_ALIGN)

        nc.vector.memset(rc_sb[0:RC_ROW, :].bitcast(I32), 0)
        nc.gpsimd.memset(scales[0:SCALE_ROW, :].bitcast(I32), 0)
        nc.gpsimd.memset(scales[SCALE_ROW + BLOCKS : P, :].bitcast(I32), 0)
        first_ident = shared.tile([P, P], F32, name="first_ident", align_bytes=ALIGN, offset=IDENT_AT)
        make_identity(nc, first_ident[:])
        second_ident = sb.tile([P, P], F32, name="second_ident")
        make_identity(nc, second_ident[:])
        listed_scales = sb.tile([P, I], U8, name="listed_scales", align_bytes=ALIGN)
        nc.gpsimd.memset(listed_scales[:].bitcast(I32), 0)

        nc.scalar.dma_start(rc_sb[RC_ROW:P, :], rc[0:1, :])
        nc.sync.dma_start(q_raw[:], by_word(query))
        nc.sync.dma_start(offs_sb[:], offs)
        nc.scalar.dma_start(scales[SCALE_ROW : SCALE_ROW + BLOCKS, :].bitcast(I32), cand_scales[0].bitcast(I32))
        o_raw = []
        for n, width in enumerate(LOADS):
            o_raw.append(shared.tile([P, PACK, width], F32, name="o_raw%d" % n, align_bytes=DMA_ALIGN, offset=RAW_AT[n]))
            nc.sync.dma_start(o_raw[n][:], by_word(other[:, LOAD_FIRST[n] : LOAD_FIRST[n] + width]))
        words = sb.tile([P, T], U16, name="words", align_bytes=DMA_ALIGN)
        nc.sync.dma_start(words[:].bitcast(I32), cand_words[0].bitcast(I32))
        nc.sync.dma_start(offs2_sb[:], offs2)

        q_cast = sb.tile([P, Q, PACK], BF16, name="q_cast", align_bytes=ALIGN)
        q_codes = sb.tile([P, Q], U32, name="q_codes", align_bytes=ALIGN)
        q_scales = sb.tile([P, Q], U8, name="q_scales", align_bytes=ALIGN)
        o_cast = [
            shared.tile([P, width, PACK], BF16, name="o_cast%d" % n, align_bytes=ALIGN, offset=CAST_AT[n])
            for n, width in enumerate(STAGE_WIDTH)
        ]
        o_codes = [sb.tile([P, c[1]], U32, name="o_codes%d" % k, align_bytes=ALIGN) for k, c in enumerate(CHUNKS)]
        o_scales = [sb.tile([P, c[1]], U8, name="o_scales%d" % k, align_bytes=ALIGN) for k, c in enumerate(CHUNKS)]
        rc_turned_ps = ps.tile([P, SLOT_TILES, P], F32, name="rc_turned_ps", tag="b_ps0")
        b_ps = [ps.tile([P, BANK], F32, name="b_ps%d" % k) for k in range(len(BANKS))]
        rc_rows_ps = ps.tile([P, I], F32, name="rc_rows_ps")
        listed_words = [
            shared.tile([P, HALF], U16, name="listed_words%d" % h, align_bytes=ALIGN, offset=at)
            for h, at in enumerate([RAW_AT[-1], RAW_AT[-1] + 2 * HALF])
        ]
        b_sb = shared.tile([P, U], F32, name="b_sb", align_bytes=ALIGN, offset=B_AT)

        def cast(stage):
            for engine, first, width in STAGES[stage]:
                load = max(n for n in range(len(LOADS)) if LOAD_FIRST[n] <= first)
                at, to = first - LOAD_FIRST[load], first - STAGE_FIRST[stage]
                copy = nc.vector.tensor_copy if engine == "vector" else nc.scalar.copy
                copy(cast_view(o_cast[stage][:, to : to + width, :]), raw_view(o_raw[load][:, :, at : at + width]))

        def score_chunk(k):
            first, width = CHUNKS[k]
            stage = max(n for n in range(len(STAGES)) if STAGE_FIRST[n] <= first)
            at = first - STAGE_FIRST[stage]
            quantise(o_codes[k][:], o_scales[k][:], o_cast[stage][:, at : at + width, :])
            bank = max(n for n in range(len(BANKS)) if BANKS[n][0] <= first)
            place = first - BANKS[bank][0]
            nc.tensor.matmul_mx(
                b_ps[bank][:, place : place + width],
                lhsT=q_codes[:].bitcast(FP8X4),
                lhsT_scale=q_scales[:],
                rhs=o_codes[k][:].bitcast(FP8X4),
                rhs_scale=o_scales[k][:],
                start=True,
                stop=True,
            )

        def empty_bank(k):
            first, width = BANKS[k]
            nc.scalar.copy(b_sb[:, first : first + width], b_ps[k][:, :width])

        listed_rc = sb.tile([P, I], F32, name="listed_rc", align_bytes=ALIGN)
        nc.vector.tensor_copy(listed_rc[:], rc_sb[:].indirect(offs_sb[:]))
        for c in range(SLOT_TILES):
            nc.tensor.transpose(rc_turned_ps[:, c, :], listed_rc[:, c * P : (c + 1) * P], first_ident[:])
        listed_scale_rows = sb.tile([P, I], U8, name="listed_scale_rows", align_bytes=ALIGN)
        nc.vector.tensor_copy(listed_scale_rows[:], scales[:].indirect(offs_sb[:]))
        for quadrant in range(P // QUADRANT):
            nc.sync.dma_start(
                listed_scales[QUADRANT * quadrant : QUADRANT * quadrant + 4, :].bitcast(I32),
                listed_scale_rows[SCALE_ROW + 4 * quadrant : SCALE_ROW + 4 * quadrant + 4, :].bitcast(I32),
            )
        nc.scalar.copy(cast_view(q_cast[:]), raw_view(q_raw[:]))
        quantise(q_codes[:], q_scales[:], q_cast[:])

        cast(0)
        rc_columns = sb.tile([P, SLOT_TILES], F32, name="rc_columns")
        nc.scalar.copy(rc_columns[:], rc_turned_ps[:, :, RC_ROW])
        score_chunk(0)
        for c in range(SLOT_TILES):
            nc.tensor.transpose(
                rc_rows_ps[:, c * P : (c + 1) * P], rc_columns[:, c : c + 1].to_broadcast([P, P]), second_ident[:]
            )
        cast(1)
        cast(2)
        empty_bank(0)
        score_chunk(1)
        score_chunk(2)
        cast(3)
        rc_rows = shared.tile([P, I], F32, name="rc_rows", align_bytes=ALIGN, offset=RAW_AT[2])
        nc.scalar.copy(rc_rows[:], rc_rows_ps[:])
        score_chunk(3)
        score_chunk(4)
        for k in range(1, len(BANKS)):
            empty_bank(k)

        halves = [slice(h * HALF, (h + 1) * HALF) for h in range(2)]
        a_ps = [ps.tile([P, BANK], F32, name="a_ps%d" % h) for h in range(2)]
        for h in range(2):
            nc.vector.tensor_copy(
                listed_words[h][:], words[:].indirect(offs_sb[:, h * HALF // 16 : (h + 1) * HALF // 16])
            )
            nc.tensor.matmul_mx(
                a_ps[h][:, :HALF],
                lhsT=q_codes[:].bitcast(FP8X4),
                lhsT_scale=q_scales[:],
                rhs=listed_words[h][:].bitcast(FP4X4),
                rhs_scale=listed_scales[:, halves[h]],
                start=True,
                stop=True,
            )

        means = [sb.tile([P, 1], F32, name="mean%d" % h) for h in range(2)]
        parts = [FIRST_LOOKUPS, J - FIRST_LOOKUPS]
        listed_b = [sb.tile([P, parts[h]], F32, name="listed_b%d" % h) for h in range(2)]
        scaled_b = [sb.tile([P, parts[h]], F32, name="scaled_b%d" % h) for h in range(2)]
        split = parts[1] - SCALAR_LOOKUPS
        nc.scalar.activation(
            listed_b[1][:, split:], b_sb[:].indirect(offs2_sb[:, (J - SCALAR_LOOKUPS) // 16 :]), ACT.Copy
        )
        nc.vector.tensor_copy(listed_b[0][:], b_sb[:].indirect(offs2_sb[:, : FIRST_LOOKUPS // 16]))
        nc.vector.tensor_copy(
            listed_b[1][:, :split], b_sb[:].indirect(offs2_sb[:, FIRST_LOOKUPS // 16 : (J - SCALAR_LOOKUPS) // 16])
        )
        for h in range(2):
            nc.scalar.activation(scaled_b[h][:], listed_b[h][:], ACT.Copy, scale=1.0 / J, accum_out=means[h][:])

        without_mean = [sb.tile([P, HALF], F32, name="without_mean%d" % h) for h in range(2)]
        for h in range(2):
            nc.vector.scalar_tensor_tensor(
                without_mean[h][:], a_ps[h][:, :HALF], 2.0, rc_rows[:, halves[h]], ALU.mult, ALU.subtract
            )
        for h in range(2):
            result = sb.tile([P, HALF], F32, name="result%d" % h, align_bytes=DMA_ALIGN)
            nc.vector.tensor_scalar(
                result[:], without_mean[h][:], means[0][:], means[1][:], ALU.subtract, ALU.subtract
            )
            nc.sync.dma_start(out[:, halves[h]], result[:])
